import numpy as np
import ml_dtypes


def mxq(x, axis, fmt="e4m3"):
    dtype, down = {"e4m3": (ml_dtypes.float8_e4m3fn, 7), "e5m2": (ml_dtypes.float8_e5m2, 14)}[fmt]
    v = np.moveaxis(np.asarray(x, np.float32).astype(ml_dtypes.bfloat16).astype(np.float64), axis, -1)
    blocks = v.reshape(v.shape[:-1] + (-1, 32))
    amax = np.abs(blocks).max(-1, keepdims=True)
    byte = np.maximum(np.where(amax > 0, np.frexp(amax)[1] - 1 + 127, 0) - down, 1)
    scale = np.exp2(byte - 127.0)
    codes = (blocks / scale).astype(np.float32).astype(dtype).astype(np.float64)
    return np.moveaxis((codes * scale).reshape(v.shape), -1, axis)


WIDE = False


def mx_kscale(k):
    if not WIDE:
        return np.ones(k)
    levels = np.array([10, -10, 5, -5, 0])
    if k % 512:
        return np.exp2(np.random.permutation(np.resize(levels, k // 32))).repeat(32)
    a = np.empty((k // 512, 16))
    for p in range(k // 512):
        a[p, :8] = np.random.permutation(np.resize(levels, 8))
        for g in range(8):
            far = levels[np.abs(levels - a[p, g]) >= 10]
            a[p, g + 8] = far[np.random.randint(len(far))]
    return np.exp2(a.ravel()).repeat(32)


BF16 = ml_dtypes.bfloat16


def bf(x):
    return np.asarray(x, np.float32).astype(BF16)


def f64(x):
    return np.asarray(x).astype(np.float64)


E2M1 = np.array([0.0, 0.5, 1.0, 1.5, 2.0, 3.0, 4.0, 6.0, -0.0, -0.5, -1.0, -1.5, -2.0, -3.0, -4.0, -6.0])


def pack_weight(w, fmt):
    k, n = w.shape
    w = f64(bf(w)).reshape(k // 32, 32, n)
    amax = np.abs(w).max(1)
    if fmt == "e4m3":
        byte = np.frexp(amax)[1] - 1 + 127 - 7
    else:
        mant, ex = np.frexp(amax / 6.0)
        byte = np.where(mant > 0.5, ex, ex - 1) + 127
    byte = np.clip(np.where(amax > 0, byte, 1), 1, 254)
    scaled = (w * np.exp2(127.0 - byte)[:, None, :]).reshape(k, n).astype(np.float32)
    by_word = np.ascontiguousarray(scaled.reshape(k // 512, 128, 4, n).transpose(0, 1, 3, 2))
    if fmt == "e4m3":
        words = by_word.astype(ml_dtypes.float8_e4m3fn).view(np.uint8)
    else:
        c = by_word.astype(ml_dtypes.float4_e2m1fn).view(np.uint8) & 0xF
        words = c[..., 0::2] | (c[..., 1::2] << 4)
    return np.ascontiguousarray(words), np.ascontiguousarray(byte.astype(np.uint8).reshape(k // 512, 16, n))


def unpack_weight(words, scales, fmt):
    g, p, n, _ = words.shape
    if fmt == "e4m3":
        vals = np.ascontiguousarray(words).view(ml_dtypes.float8_e4m3fn).astype(np.float64)
    else:
        nib = np.empty((g, p, n, 4), np.uint8)
        nib[..., 0::2] = words & 0xF
        nib[..., 1::2] = words >> 4
        vals = E2M1[nib]
    vals = vals * np.repeat(np.exp2(scales.astype(np.float64) - 127.0), 8, axis=1)[..., None]
    return vals.transpose(0, 1, 3, 2).reshape(g * 512, n)
def pack4(w):
    words, scales = pack_weight(w, "e2m1")
    return words.reshape(words.shape[0], 128, -1), scales


def unpack4(words, scales):
    return unpack_weight(words.reshape(words.shape[0], 128, -1, 2), scales, "e2m1")


def planes(Y):
    n, m = Y.shape
    b = f64(bf(Y)).reshape(n // 32, 32, m)
    amax = np.abs(b).max(1)
    byte = np.clip(np.where(amax > 0, np.frexp(amax)[1] - 1 + 127 - 7, 1), 1, 254)
    codes = (b * np.exp2(127.0 - byte)[:, None, :]).reshape(n, m).astype(np.float32).astype(ml_dtypes.float8_e4m3fn).view(np.uint8)
    words = codes.reshape(n // 512, 128, 4, m).transpose(0, 1, 3, 2)
    return np.ascontiguousarray(words), np.ascontiguousarray(byte.astype(np.uint8).reshape(n // 512, 16, m))


Q, H, DH, K, KO = 512, 4, 512, 3584, 512


def setup_inputs():
    s = mx_kscale(K)
    so = mx_kscale(KO)
    spread = np.exp(0.8 * np.random.randn(DH))
    cols = np.tile(spread, H)
    queries = np.random.randn(Q, K)
    queries_outlier = 3.0 * np.random.randn(Q, KO)
    w = 0.7 * np.random.randn(K, H * DH) / np.sqrt(K + KO) * cols
    w_outlier = 0.7 * np.random.randn(KO, H * DH) / np.sqrt(K + KO) * cols
    wq_words, wq_scales = pack4(w / s[:, None])
    return {
        "queries": bf(queries * s),
        "queries_outlier": bf(queries_outlier * so),
        "wq_words": wq_words,
        "wq_scales": wq_scales,
        "w_outlier": bf(w_outlier / so[:, None]),
        "bias": bf(0.4 * np.random.randn(H * DH) * cols),
        "pos": bf(0.4 * np.random.randn(Q, DH) * spread),
        "head_scale": bf(np.exp(0.5 * np.random.randn(H))),
    }

def reference(queries, queries_outlier, wq_words, wq_scales, w_outlier, bias, pos, head_scale):
    main = mxq(f64(queries), 1, "e4m3") @ unpack4(wq_words, wq_scales)
    outlier = mxq(f64(queries_outlier), 1, "e4m3") @ mxq(f64(w_outlier), 0, "e4m3")
    proj = (main + outlier + f64(bias)).reshape(Q, H, DH).transpose(1, 0, 2)
    y = (proj + f64(pos)) * f64(head_scale).reshape(H, 1, 1)
    Y = y.transpose(2, 0, 1).reshape(DH, H * Q)
    words, scales = planes(Y)
    return y, words, scales

@@ -1,0 +1,391 @@
+from contextlib import ExitStack
+
+import concourse.mybir as mybir
+from concourse.masks import make_identity
+
+Q, H, DH, K, KO = 512, 4, 512, 3584, 512
+FLOPS = 2 * Q * (K + KO) * H * DH
+
+F32 = mybir.dt.float32
+BF16 = mybir.dt.bfloat16
+I32 = mybir.dt.int32
+U32 = mybir.dt.uint32
+U8 = mybir.dt.uint8
+FP8X4 = mybir.dt.float8_e4m3fn_x4
+FP4X4 = mybir.dt.float4_e2m1fn_x4
+MULT = mybir.AluOpType.mult
+ADD = mybir.AluOpType.add
+
+P = 128
+UT = Q // P
+G_MAIN = K // 512
+PASSES = G_MAIN + 1
+STEPS = 8
+
+
+def tile_resampler_query_projection_g5_kernel(
+    tc, queries, queries_outlier, wq_words, wq_scales, w_outlier, bias, pos, head_scale, out_0, out_1, out_2
+):
+    nc = tc.nc
+    with ExitStack() as ctx:
+        keep = ctx.enter_context(tc.tile_pool(name="keep", bufs=1))
+        psum = ctx.enter_context(tc.psum_pool(name="psum", bufs=1))
+        ctx.enter_context(tc.manual_schedule())
+
+        def sb(name, shape, dtype):
+            return keep.tile(shape, dtype, name=name, align_bytes=64)
+
+        bank = [psum.tile([P, 512], F32, name="bank%d" % i) for i in range(8)]
+
+        ident = sb("ident", [P, P], F32)
+        bias_col = sb("bias_col", [P, H, 4], BF16)
+        hs_bf = sb("hs_bf", [P, H], BF16)
+        hs = sb("hs", [P, H], F32)
+        bias_bc = sb("bias_bc", [P, H, DH], BF16)
+        bias_hs = sb("bias_hs", [P, H, DH], F32)
+        pos_sb = sb("pos_sb", [P, UT, DH], BF16)
+        x_raw = [sb("x_raw%d" % s, [P, 2, 1024], BF16) for s in range(STEPS)]
+        x_perm = [sb("x_perm%d" % i, [P, 4, 2, P], F32) for i in range(2)]
+        x_grp = [sb("x_grp%d" % i, [P, 2, 1024], BF16) for i in range(2)]
+        x_codes = sb("x_codes", [P, UT, PASSES * P], U32)
+        x_scales = sb("x_scales", [P, UT, PASSES * P], U8)
+        w_words = [sb("w_words%d" % h, [P, G_MAIN, 2 * DH], U8) for h in range(H)]
+        w_scales01 = [sb("w_scales%d" % h, [P, G_MAIN, DH], U8) for h in range(2)]
+        w_scales23 = sb("w_scales23", [P, G_MAIN, 2 * DH], U8)
+        wo_raw = [sb("wo_raw%d" % h, [P, 4, DH], BF16) for h in range(H)]
+        wo_grp = [sb("wo_grp%d" % i, [P, DH, 4], BF16) for i in range(2)]
+        wo_codes = sb("wo_codes", [P, H, DH], U32)
+        wo_scales = sb("wo_scales", [P, H, DH], U8)
+        addend = [sb("addend%d" % i, [P, UT, DH], F32) for i in range(2)]
+        y = [sb("y%d" % h, [P, UT, DH], F32) for h in range(3)]
+        y_bf = [sb("y_bf%d" % i, [P, UT, 2, P, 2], BF16) for i in range(2)]
+        y_grp = [sb("y_grp%d" % i, [P, UT, DH], BF16) for i in range(2)]
+        y_codes = sb("y_codes", [P, H * Q], U32)
+        y_scales = sb("y_scales", [P, H * Q], U8)
+
+        make_identity(nc, ident[:])
+        nc.scalar.dma_start(out=bias_col[:], in_=bias.rearrange("(h p j) -> p h j", h=H, j=4))
+        nc.scalar.dma_start(out=hs_bf[:], in_=head_scale.partition_broadcast(P))
+        nc.vector.memset(w_scales01[0][:].bitcast(I32), 0)
+        nc.vector.memset(w_scales01[1][:].bitcast(I32), 0)
+        nc.vector.memset(w_scales23[:].bitcast(I32), 0)
+
+        x_hbm = queries.rearrange("(a p) k -> p a k", p=P)
+        xo_hbm = queries_outlier.rearrange("(a p) k -> p a k", p=P)
+        ww_hbm = wq_words.bitcast(I32).rearrange("g p c -> p g c")
+        ws_hbm = wq_scales.bitcast(I32).rearrange("g (q r) c -> r q g c", r=4)
+        wo_hbm = w_outlier.rearrange("(p j) c -> p j c", j=4)
+
+        def load_x(s):
+            a0, k0 = 2 * (s % 2), 1024 * (s // 2)
+            if s == 0:
+                for a in range(2):
+                    nc.sync.dma_start(out=x_raw[s][:, a, :], in_=x_hbm[:, a, 0:1024])
+            elif k0 + 1024 <= K:
+                nc.sync.dma_start(out=x_raw[s][:], in_=x_hbm[:, a0 : a0 + 2, k0 : k0 + 1024])
+            else:
+                nc.sync.dma_start(out=x_raw[s][:, :, 0:512], in_=x_hbm[:, a0 : a0 + 2, k0:K])
+                nc.sync.dma_start(out=x_raw[s][:, :, 512:1024], in_=xo_hbm[:, a0 : a0 + 2, :])
+
+        def load_w(h, g0, g1):
+            nc.sync.dma_start(out=w_words[h][:].bitcast(I32)[:, g0:g1, :], in_=ww_hbm[:, g0:g1, 256 * h : 256 * (h + 1)])
+
+        def load_ws(tile, c0, c1, g0, g1):
+            view = tile[:].bitcast(I32)
+            for r in range(4):
+                nc.sync.dma_start(out=view[r:P:32, g0:g1, :], in_=ws_hbm[r][:, g0:g1, c0 // 4 : c1 // 4])
+
+        def load_wo(h):
+            nc.sync.dma_start(out=wo_raw[h][:], in_=wo_hbm[:, :, DH * h : DH * (h + 1)])
+
+        load_x(0)
+        load_x(1)
+        load_ws(w_scales01[0], 0, 512, 0, 2)
+        load_w(0, 0, 2)
+        load_x(2)
+        load_ws(w_scales01[0], 0, 512, 2, 7)
+        load_w(0, 2, 4)
+        load_x(3)
+        load_x(4)
+        load_w(0, 4, 7)
+        load_x(5)
+        load_wo(0)
+        load_x(6)
+        load_x(7)
+        nc.sync.dma_start(out=pos_sb[:], in_=pos.rearrange("(a p) d -> p a d", p=P))
+        load_ws(w_scales01[1], 512, 1024, 0, 7)
+        load_w(1, 0, 3)
+        load_w(1, 3, 7)
+        load_wo(1)
+        load_ws(w_scales23, 1024, 2048, 0, 7)
+        load_w(2, 0, 7)
+        load_wo(2)
+        load_w(3, 0, 7)
+        load_wo(3)
+
+        nc.vector.tensor_copy(out=hs[:], in_=hs_bf[:])
+
+        bias_words = bias_col[:].bitcast(F32)
+        for h in range(H):
+            for j in range(2):
+                q = 2 * (h % 2) + j
+                nc.tensor.transpose(
+                    bank[2 + h // 2][:, P * q : P * (q + 1)], bias_words[:, h, j : j + 1].to_broadcast([P, P]), ident[:]
+                )
+        for b in range(2):
+            nc.scalar.copy(
+                out=bias_bc[:, 2 * b : 2 * b + 2, :].bitcast(F32).rearrange("p h (n j) -> p h n j", j=2),
+                in_=bank[2 + b][:].rearrange("p (h j n) -> p h n j", h=2, j=2),
+            )
+
+        def x_permute(s, a0, a1):
+            words = x_raw[s][:, a0:a1, :].bitcast(F32).rearrange("p a (g w j) -> p (a g) j w", g=2, j=2)
+            nc.vector.tensor_copy(out=x_perm[s % 2][:, 2 * a0 : 2 * a1, :, :], in_=words)
+
+        def x_transpose(s, a):
+            dst = bank[4 + 2 * (s % 2) + a]
+            for g in range(2):
+                for j in range(2):
+                    q = 2 * g + j
+                    nc.tensor.transpose(dst[:, P * q : P * (q + 1)], x_perm[s % 2][:, 2 * a + g, j, :], ident[:])
+
+        def x_drain(s, a):
+            nc.scalar.copy(
+                out=x_grp[s % 2][:, a, :].bitcast(F32).rearrange("p (g u j) -> p g u j", g=2, j=2),
+                in_=bank[4 + 2 * (s % 2) + a][:].rearrange("p (g j u) -> p g u j", g=2, j=2),
+            )
+
+        def x_quantize(s, a):
+            ut, c0 = 2 * (s % 2) + a, 2 * P * (s // 2)
+            nc.vector.quantize_mx(
+                out=x_codes[:, ut, c0 : c0 + 2 * P].bitcast(FP8X4),
+                scales=x_scales[:, ut, c0 : c0 + 2 * P],
+                in_=x_grp[s % 2][:, a, :],
+            )
+
+        def wo_group(h, c0, c1, on_vector):
+            dst = wo_grp[h % 2][:, c0:c1, :]
+            src = wo_raw[h][:, :, c0:c1].rearrange("p j c -> p c j")
+            if on_vector:
+                nc.vector.tensor_copy(out=dst, in_=src)
+            else:
+                nc.scalar.copy(out=dst, in_=src)
+
+        def wo_quantize(h):
+            nc.vector.quantize_mx(
+                out=wo_codes[:, h, :].bitcast(FP8X4),
+                scales=wo_scales[:, h, :],
+                in_=wo_grp[h % 2][:].rearrange("p c j -> p (c j)"),
+            )
+
+        acc_bank = [[0, 1, 2, 3], [4, 5, 6, 7], [2, 3, 0, 1], [6, 7, 4, 5]]
+
+        def mx_pass(h, ut, g):
+            if g < G_MAIN:
+                rhs = w_words[h][:, g, :].bitcast(FP4X4)
+                rhs_scale = w_scales01[h][:, g, :] if h < 2 else w_scales23[:, g, DH * (h - 2) : DH * (h - 1)]
+            else:
+                rhs = wo_codes[:, h, :].bitcast(FP8X4)
+                rhs_scale = wo_scales[:, h, :]
+            nc.tensor.matmul_mx(
+                out=bank[acc_bank[h][ut]][:],
+                lhsT=x_codes[:, ut, P * g : P * (g + 1)].bitcast(FP8X4),
+                lhsT_scale=x_scales[:, ut, P * g : P * (g + 1)],
+                rhs=rhs,
+                rhs_scale=rhs_scale,
+                start=(g == 0),
+                stop=(g == PASSES - 1),
+            )
+
+        def step_matmuls(s):
+            for g in range(2 * (s // 2), 2 * (s // 2) + 2):
+                for a in range(2):
+                    mx_pass(0, 2 * (s % 2) + a, g)
+
+        def group_matmuls(h, ut):
+            for g in range(PASSES):
+                mx_pass(h, ut, g)
+
+        def scale_bias(h):
+            nc.vector.tensor_scalar(
+                out=bias_hs[:, h, :], in0=bias_bc[:, h, :], scalar1=hs[:, h : h + 1], scalar2=None, op0=MULT
+            )
+
+        def make_addend(h, ut):
+            nc.vector.scalar_tensor_tensor(
+                out=addend[h % 2][:, ut, :], in0=pos_sb[:, ut, :], scalar=hs[:, h : h + 1], in1=bias_hs[:, h, :],
+                op0=MULT, op1=ADD,
+            )
+
+        def finish(h, ut):
+            nc.vector.scalar_tensor_tensor(
+                out=y[h % 3][:, ut, :], in0=bank[acc_bank[h][ut]][:], scalar=hs[:, h : h + 1], in1=addend[h % 2][:, ut, :],
+                op0=MULT, op1=ADD,
+            )
+            nc.sync.dma_start(out=out_0[h, P * ut : P * (ut + 1), :], in_=y[h % 3][:, ut, :])
+
+        def finish_bf16(h, ut):
+            acc = bank[acc_bank[h][ut]][:].rearrange("p (w j e) -> p j w e", j=2, e=2)
+            add = addend[h % 2][:, ut, :].rearrange("p (w j e) -> p j w e", j=2, e=2)
+            for j in range(2):
+                nc.vector.scalar_tensor_tensor(
+                    out=y_bf[h % 2][:, ut, j, :, :], in0=acc[:, j, :, :], scalar=hs[:, h : h + 1], in1=add[:, j, :, :],
+                    op0=MULT, op1=ADD,
+                )
+
+        def y_round(h, ut):
+            nc.scalar.copy(
+                out=y_bf[h % 2][:, ut, :, :, :], in_=y[h % 3][:, ut, :].rearrange("p (w j e) -> p j w e", j=2, e=2)
+            )
+
+        def y_transpose(h, u0, u1, b):
+            for ut in range(u0, u1):
+                for j in range(2):
+                    q = 2 * (ut - u0) + j
+                    words = y_bf[h % 2][:, ut, j, :, :].rearrange("p w e -> p (w e)").bitcast(F32)
+                    nc.tensor.transpose(bank[b][:, P * q : P * (q + 1)], words, ident[:])
+
+        def y_drain(h, u0, u1, b):
+            n = u1 - u0
+            nc.scalar.copy(
+                out=y_grp[h % 2][:, u0:u1, :].bitcast(F32).rearrange("p a (u j) -> p a u j", j=2),
+                in_=bank[b][:, 0 : 2 * P * n].rearrange("p (a j u) -> p a u j", a=n, j=2),
+            )
+
+        def y_quantize(h, u0, u1):
+            c0, c1 = Q * h + P * u0, Q * h + P * u1
+            nc.vector.quantize_mx(
+                out=y_codes[:, c0:c1].bitcast(FP8X4),
+                scales=y_scales[:, c0:c1],
+                in_=y_grp[h % 2][:, u0:u1, :].rearrange("p a c -> p (a c)"),
+            )
+
+        words_hbm = out_1[0].rearrange("p m t -> p (m t)").bitcast(I32)
+        scales_hbm = out_2[0].bitcast(I32).rearrange("(q r) c -> r q c", r=4)
+
+        def store_words(c0, c1):
+            nc.sync.dma_start(out=words_hbm[:, c0:c1], in_=y_codes[:, c0:c1].bitcast(I32))
+
+        def store_scales(c0, c1, queues):
+            view = y_scales[:].bitcast(I32)
+            for r in range(4):
+                queues[r].dma_start(out=scales_hbm[r][:, c0 // 4 : c1 // 4], in_=view[r:P:32, c0 // 4 : c1 // 4])
+
+        for a in range(2):
+            x_permute(0, a, a + 1)
+            x_transpose(0, a)
+            x_drain(0, a)
+        x_permute(1, 0, 2)
+        for s in range(STEPS):
+            if s + 1 < STEPS:
+                for a in range(2):
+                    x_transpose(s + 1, a)
+                    x_drain(s + 1, a)
+            for a in range(2):
+                x_quantize(s, a)
+            if s + 2 < STEPS:
+                x_permute(s + 2, 0, 2)
+            if s == 3:
+                wo_group(0, 0, 128, False)
+            if s == 4:
+                wo_group(0, 128, 256, False)
+                wo_group(0, 256, 512, True)
+            if s == 5:
+                wo_quantize(0)
+            if s == 6:
+                scale_bias(0)
+            step_matmuls(s)
+
+        for ut in range(UT):
+            make_addend(0, ut)
+        for ut in range(UT):
+            finish(0, ut)
+            y_round(0, ut)
+        for g in range(4):
+            for ut in range(UT):
+                mx_pass(1, ut, g)
+        y_transpose(0, 0, 2, 0)
+        y_transpose(0, 2, 4, 1)
+        scale_bias(1)
+        scale_bias(2)
+        for ut in range(UT):
+            make_addend(1, ut)
+        wo_group(1, 0, 512, False)
+        make_addend(2, 0)
+        wo_quantize(1)
+        for g in range(4, PASSES):
+            for ut in range(UT):
+                mx_pass(1, ut, g)
+        y_drain(0, 0, 2, 0)
+        y_drain(0, 2, 4, 1)
+        make_addend(2, 1)
+        y_quantize(0, 0, 4)
+        store_words(0, Q)
+        make_addend(2, 2)
+        make_addend(2, 3)
+        wo_group(2, 0, 512, False)
+
+        finish(1, 0)
+        y_round(1, 0)
+        wo_quantize(2)
+        for ut in range(1, UT):
+            finish(1, ut)
+            y_round(1, ut)
+        group_matmuls(2, 0)
+        group_matmuls(2, 1)
+        y_transpose(1, 0, 2, 4)
+        y_transpose(1, 2, 4, 5)
+        finish(2, 0)
+        y_round(2, 0)
+        scale_bias(3)
+        wo_group(3, 0, 256, False)
+        make_addend(3, 0)
+        finish(2, 1)
+        y_drain(1, 0, 2, 4)
+        y_drain(1, 2, 4, 5)
+        y_round(2, 1)
+        wo_group(3, 256, 512, False)
+        make_addend(3, 1)
+        y_quantize(1, 0, 4)
+        store_words(Q, 2 * Q)
+        group_matmuls(2, 2)
+        make_addend(3, 2)
+        finish(2, 2)
+        y_round(2, 2)
+        wo_quantize(3)
+        make_addend(3, 3)
+        group_matmuls(2, 3)
+        finish(2, 3)
+        y_round(2, 3)
+
+        group_matmuls(3, 0)
+        y_transpose(2, 0, 2, 2)
+        y_transpose(2, 2, 4, 3)
+        finish(3, 0)
+        y_round(3, 0)
+        y_drain(2, 0, 2, 2)
+        y_drain(2, 2, 4, 3)
+        group_matmuls(3, 1)
+        y_quantize(2, 0, 4)
+        store_words(2 * Q, 3 * Q)
+        store_scales(0, 3 * Q, [nc.sync] * 4)
+        finish(3, 1)
+        y_round(3, 1)
+        group_matmuls(3, 2)
+        finish(3, 2)
+        y_round(3, 2)
+        group_matmuls(3, 3)
+        y_transpose(3, 0, 2, 0)
+        y_transpose(3, 2, 3, 1)
+        finish_bf16(3, 3)
+        y_transpose(3, 3, 4, 2)
+        finish(3, 3)
+        y_drain(3, 0, 2, 0)
+        y_drain(3, 2, 3, 1)
+        y_drain(3, 3, 4, 2)
+        y_quantize(3, 0, 2)
+        y_quantize(3, 2, 3)
+        store_words(3 * Q, 3 * Q + 3 * P)
+        y_quantize(3, 3, 4)
+        store_words(3 * Q + 3 * P, 4 * Q)
+        store_scales(3 * Q, 4 * Q, [nc.scalar, nc.sync, nc.scalar, nc.sync])

@@ -78,9 +78,9 @@ def tile_resampler_query_projection_g5_kernel(
 
         def load_x(s):
             a0, k0 = 2 * (s % 2), 1024 * (s // 2)
-            if s == 0:
+            if s < 2:
                 for a in range(2):
-                    nc.sync.dma_start(out=x_raw[s][:, a, :], in_=x_hbm[:, a, 0:1024])
+                    nc.sync.dma_start(out=x_raw[s][:, a, :], in_=x_hbm[:, a0 + a, 0:1024])
             elif k0 + 1024 <= K:
                 nc.sync.dma_start(out=x_raw[s][:], in_=x_hbm[:, a0 : a0 + 2, k0 : k0 + 1024])
             else:
@@ -103,19 +103,19 @@ def tile_resampler_query_projection_g5_kernel(
         load_ws(w_scales01[0], 0, 512, 0, 2)
         load_w(0, 0, 2)
         load_x(2)
+        load_x(3)
         load_ws(w_scales01[0], 0, 512, 2, 7)
         load_w(0, 2, 4)
-        load_x(3)
         load_x(4)
-        load_w(0, 4, 7)
         load_x(5)
-        load_wo(0)
+        load_w(0, 4, 7)
         load_x(6)
         load_x(7)
-        nc.sync.dma_start(out=pos_sb[:], in_=pos.rearrange("(a p) d -> p a d", p=P))
         load_ws(w_scales01[1], 512, 1024, 0, 7)
         load_w(1, 0, 3)
+        load_wo(0)
         load_w(1, 3, 7)
+        nc.sync.dma_start(out=pos_sb[:], in_=pos.rearrange("(a p) d -> p a d", p=P))
         load_wo(1)
         load_ws(w_scales23, 1024, 2048, 0, 7)
         load_w(2, 0, 7)
@@ -124,6 +124,9 @@ def tile_resampler_query_projection_g5_kernel(
         load_wo(3)
 
         nc.vector.tensor_copy(out=hs[:], in_=hs_bf[:])
+
+        for q in range(6):
+            nc.tensor.transpose(bank[q // 4][:, P * (q % 4) : P * (q % 4 + 1)], ident[:], ident[:])
 
         bias_words = bias_col[:].bitcast(F32)
         for h in range(H):
@@ -271,66 +274,69 @@ def tile_resampler_query_projection_g5_kernel(
             for r in range(4):
                 queues[r].dma_start(out=scales_hbm[r][:, c0 // 4 : c1 // 4], in_=view[r:P:32, c0 // 4 : c1 // 4])
 
-        for a in range(2):
-            x_permute(0, a, a + 1)
-            x_transpose(0, a)
-            x_drain(0, a)
-        x_permute(1, 0, 2)
-        for s in range(STEPS):
-            if s + 1 < STEPS:
-                for a in range(2):
-                    x_transpose(s + 1, a)
-                    x_drain(s + 1, a)
-            for a in range(2):
-                x_quantize(s, a)
-            if s + 2 < STEPS:
-                x_permute(s + 2, 0, 2)
-            if s == 3:
-                wo_group(0, 0, 128, False)
-            if s == 4:
-                wo_group(0, 128, 256, False)
-                wo_group(0, 256, 512, True)
-            if s == 5:
-                wo_quantize(0)
-            if s == 6:
-                scale_bias(0)
-            step_matmuls(s)
+        def pair_matmuls(pair, ut):
+            for g in range(2 * pair, min(2 * pair + 2, G_MAIN)):
+                mx_pass(0, ut, g)
 
+        for ut in range(UT):
+            x_permute(ut // 2, ut % 2, ut % 2 + 1)
+        for pair in range(4):
+            for ut in range(UT):
+                x_transpose(2 * pair + ut // 2, ut % 2)
+                x_drain(2 * pair + ut // 2, ut % 2)
+            if pair > 0:
+                pair_matmuls(pair - 1, 3)
+            for ut in range(3):
+                x_quantize(2 * pair + ut // 2, ut % 2)
+                pair_matmuls(pair, ut)
+            if pair < 3:
+                x_permute(2 * pair + 2, 0, 2)
+                x_permute(2 * pair + 3, 0, 2)
+            x_quantize(2 * pair + 1, 1)
+        mx_pass(1, 0, 0)
+        mx_pass(1, 1, 0)
+        pair_matmuls(3, 3)
+        mx_pass(1, 2, 0)
+        mx_pass(1, 3, 0)
+
+        def sweep(h, g0, g1):
+            for g in range(g0, g1):
+                for ut in range(UT):
+                    mx_pass(h, ut, g)
+
+        scale_bias(0)
+        scale_bias(1)
+        wo_group(0, 0, 256, False)
+        wo_group(0, 256, 512, True)
+        scale_bias(2)
+        wo_quantize(0)
+        sweep(1, 1, 2)
+        sweep(0, G_MAIN, PASSES)
+        sweep(1, 2, G_MAIN)
+        wo_group(1, 0, 512, False)
         for ut in range(UT):
             make_addend(0, ut)
         for ut in range(UT):
             finish(0, ut)
             y_round(0, ut)
-        for g in range(4):
-            for ut in range(UT):
-                mx_pass(1, ut, g)
+        wo_quantize(1)
+        sweep(1, G_MAIN, PASSES)
         y_transpose(0, 0, 2, 0)
         y_transpose(0, 2, 4, 1)
-        scale_bias(1)
-        scale_bias(2)
         for ut in range(UT):
             make_addend(1, ut)
-        wo_group(1, 0, 512, False)
-        make_addend(2, 0)
-        wo_quantize(1)
-        for g in range(4, PASSES):
-            for ut in range(UT):
-                mx_pass(1, ut, g)
+        wo_group(2, 0, 512, False)
         y_drain(0, 0, 2, 0)
         y_drain(0, 2, 4, 1)
+        make_addend(2, 0)
         make_addend(2, 1)
-        y_quantize(0, 0, 4)
-        store_words(0, Q)
-        make_addend(2, 2)
-        make_addend(2, 3)
-        wo_group(2, 0, 512, False)
 
-        finish(1, 0)
-        y_round(1, 0)
         wo_quantize(2)
-        for ut in range(1, UT):
+        for ut in range(UT):
             finish(1, ut)
             y_round(1, ut)
+        y_quantize(0, 0, 4)
+        store_words(0, Q)
         group_matmuls(2, 0)
         group_matmuls(2, 1)
         y_transpose(1, 0, 2, 4)
@@ -339,8 +345,10 @@ def tile_resampler_query_projection_g5_kernel(
         y_round(2, 0)
         scale_bias(3)
         wo_group(3, 0, 256, False)
-        make_addend(3, 0)
+        make_addend(2, 2)
         finish(2, 1)
+        make_addend(2, 3)
+        make_addend(3, 0)
         y_drain(1, 0, 2, 4)
         y_drain(1, 2, 4, 5)
         y_round(2, 1)

@@ -21,6 +21,7 @@ UT = Q // P
 G_MAIN = K // 512
 PASSES = G_MAIN + 1
 STEPS = 8
+WARM_PASSES = 7
 
 
 def tile_resampler_query_projection_g5_kernel(
@@ -38,9 +39,12 @@ def tile_resampler_query_projection_g5_kernel(
         bank = [psum.tile([P, 512], F32, name="bank%d" % i) for i in range(8)]
 
         ident = sb("ident", [P, P], F32)
-        bias_col = sb("bias_col", [P, H, 4], BF16)
+        bias_col = sb("bias_col", [P, 16], BF16)
         hs_bf = sb("hs_bf", [P, H], BF16)
         hs = sb("hs", [P, H], F32)
+        warm_in = sb("warm_in", [P, 8 * P], BF16)
+        warm_codes = sb("warm_codes", [P, 2 * P], U32)
+        warm_scales = sb("warm_scales", [P, 2 * P], U8)
         bias_bc = sb("bias_bc", [P, H, DH], BF16)
         bias_hs = sb("bias_hs", [P, H, DH], F32)
         pos_sb = sb("pos_sb", [P, UT, DH], BF16)
@@ -50,8 +54,9 @@ def tile_resampler_query_projection_g5_kernel(
         x_codes = sb("x_codes", [P, UT, PASSES * P], U32)
         x_scales = sb("x_scales", [P, UT, PASSES * P], U8)
         w_words = [sb("w_words%d" % h, [P, G_MAIN, 2 * DH], U8) for h in range(H)]
-        w_scales01 = [sb("w_scales%d" % h, [P, G_MAIN, DH], U8) for h in range(2)]
-        w_scales23 = sb("w_scales23", [P, G_MAIN, 2 * DH], U8)
+        w_scales0a = sb("w_scales0a", [P, 2, DH], U8)
+        w_scales0b = sb("w_scales0b", [P, G_MAIN - 2, DH], U8)
+        w_scales = [None] + [sb("w_scales%d" % h, [P, G_MAIN, DH], U8) for h in range(1, H)]
         wo_raw = [sb("wo_raw%d" % h, [P, 4, DH], BF16) for h in range(H)]
         wo_grp = [sb("wo_grp%d" % i, [P, DH, 4], BF16) for i in range(2)]
         wo_codes = sb("wo_codes", [P, H, DH], U32)
@@ -61,14 +66,16 @@ def tile_resampler_query_projection_g5_kernel(
         y_bf = [sb("y_bf%d" % i, [P, UT, 2, P, 2], BF16) for i in range(2)]
         y_grp = [sb("y_grp%d" % i, [P, UT, DH], BF16) for i in range(2)]
         y_codes = sb("y_codes", [P, H * Q], U32)
-        y_scales = sb("y_scales", [P, H * Q], U8)
+        y_scales = [sb("y_scales_first", [P, 3 * Q], U8), sb("y_scales_last", [P, Q], U8)]
 
         make_identity(nc, ident[:])
-        nc.scalar.dma_start(out=bias_col[:], in_=bias.rearrange("(h p j) -> p h j", h=H, j=4))
+        nc.scalar.dma_start(out=bias_col[:], in_=bias.rearrange("(p j) -> p j", p=P))
         nc.scalar.dma_start(out=hs_bf[:], in_=head_scale.partition_broadcast(P))
-        nc.vector.memset(w_scales01[0][:].bitcast(I32), 0)
-        nc.vector.memset(w_scales01[1][:].bitcast(I32), 0)
-        nc.vector.memset(w_scales23[:].bitcast(I32), 0)
+        nc.vector.memset(warm_in[:].bitcast(I32), 0)
+        nc.vector.memset(w_scales0a[:].bitcast(I32), 0)
+        nc.vector.quantize_mx(out=warm_codes[:].bitcast(FP8X4), scales=warm_scales[:], in_=warm_in[:])
+        nc.vector.memset(w_scales0b[:].bitcast(I32), 0)
+        nc.vector.memset(w_scales[1][:].bitcast(I32), 0)
 
         x_hbm = queries.rearrange("(a p) k -> p a k", p=P)
         xo_hbm = queries_outlier.rearrange("(a p) k -> p a k", p=P)
@@ -93,57 +100,63 @@ def tile_resampler_query_projection_g5_kernel(
         def load_ws(tile, c0, c1, g0, g1):
             view = tile[:].bitcast(I32)
             for r in range(4):
-                nc.sync.dma_start(out=view[r:P:32, g0:g1, :], in_=ws_hbm[r][:, g0:g1, c0 // 4 : c1 // 4])
+                nc.sync.dma_start(out=view[r:P:32, :, :], in_=ws_hbm[r][:, g0:g1, c0 // 4 : c1 // 4])
 
         def load_wo(h):
             nc.sync.dma_start(out=wo_raw[h][:], in_=wo_hbm[:, :, DH * h : DH * (h + 1)])
 
         load_x(0)
         load_x(1)
-        load_ws(w_scales01[0], 0, 512, 0, 2)
+        load_ws(w_scales0a, 0, 512, 0, 2)
         load_w(0, 0, 2)
         load_x(2)
         load_x(3)
-        load_ws(w_scales01[0], 0, 512, 2, 7)
+        load_ws(w_scales0b, 0, 512, 2, 7)
         load_w(0, 2, 4)
         load_x(4)
         load_x(5)
         load_w(0, 4, 7)
         load_x(6)
         load_x(7)
-        load_ws(w_scales01[1], 512, 1024, 0, 7)
+        load_ws(w_scales[1], 512, 1024, 0, 7)
         load_w(1, 0, 3)
         load_wo(0)
         load_w(1, 3, 7)
         nc.sync.dma_start(out=pos_sb[:], in_=pos.rearrange("(a p) d -> p a d", p=P))
         load_wo(1)
-        load_ws(w_scales23, 1024, 2048, 0, 7)
-        load_w(2, 0, 7)
-        load_wo(2)
-        load_w(3, 0, 7)
-        load_wo(3)
 
         nc.vector.tensor_copy(out=hs[:], in_=hs_bf[:])
 
-        for q in range(6):
-            nc.tensor.transpose(bank[q // 4][:, P * (q % 4) : P * (q % 4 + 1)], ident[:], ident[:])
-
-        bias_words = bias_col[:].bitcast(F32)
-        for h in range(H):
-            for j in range(2):
-                q = 2 * (h % 2) + j
-                nc.tensor.transpose(
-                    bank[2 + h // 2][:, P * q : P * (q + 1)], bias_words[:, h, j : j + 1].to_broadcast([P, P]), ident[:]
-                )
-        for b in range(2):
-            nc.scalar.copy(
-                out=bias_bc[:, 2 * b : 2 * b + 2, :].bitcast(F32).rearrange("p h (n j) -> p h n j", j=2),
-                in_=bank[2 + b][:].rearrange("p (h j n) -> p h n j", h=2, j=2),
+        def warm_pass(q):
+            nc.tensor.matmul_mx(
+                out=bank[2 + q // 2 % 2][:, 2 * P * (q % 2) : 2 * P * (q % 2 + 1)],
+                lhsT=warm_codes[:, 0:P].bitcast(FP8X4), lhsT_scale=warm_scales[:, 0:P],
+                rhs=warm_codes[:].bitcast(FP8X4), rhs_scale=warm_scales[:],
+                start=True, stop=True,
             )
 
-        def x_permute(s, a0, a1):
+        for q in range(WARM_PASSES):
+            warm_pass(q)
+
+        def spread_bias():
+            bias_words = bias_col[:].bitcast(F32)
+            bias_bc_words = bias_bc[:].rearrange("p h d -> p (h d)").bitcast(F32).rearrange("p (n j) -> p n j", j=8)
+            for b in range(2):
+                for q in range(4):
+                    j = 4 * b + q
+                    nc.tensor.transpose(
+                        bank[2 + b][:, P * q : P * (q + 1)], bias_words[:, j : j + 1].to_broadcast([P, P]), ident[:]
+                    )
+                nc.scalar.copy(
+                    out=bias_bc_words[:, :, 4 * b : 4 * b + 4], in_=bank[2 + b][:].rearrange("p (j n) -> p n j", j=4)
+                )
+
+        def x_permute(s, a0, a1, on_vector=True):
             words = x_raw[s][:, a0:a1, :].bitcast(F32).rearrange("p a (g w j) -> p (a g) j w", g=2, j=2)
-            nc.vector.tensor_copy(out=x_perm[s % 2][:, 2 * a0 : 2 * a1, :, :], in_=words)
+            if on_vector:
+                nc.vector.tensor_copy(out=x_perm[s % 2][:, 2 * a0 : 2 * a1, :, :], in_=words)
+            else:
+                nc.scalar.copy(out=x_perm[s % 2][:, 2 * a0 : 2 * a1, :, :], in_=words)
 
         def x_transpose(s, a):
             dst = bank[4 + 2 * (s % 2) + a]
@@ -181,12 +194,15 @@ def tile_resampler_query_projection_g5_kernel(
                 in_=wo_grp[h % 2][:].rearrange("p c j -> p (c j)"),
             )
 
-        acc_bank = [[0, 1, 2, 3], [4, 5, 6, 7], [2, 3, 0, 1], [6, 7, 4, 5]]
+        acc_bank = [[0, 1, 2, 3], [4, 5, 6, 7], [2, 3, 6, 7], [0, 1, 4, 5]]
 
         def mx_pass(h, ut, g):
             if g < G_MAIN:
                 rhs = w_words[h][:, g, :].bitcast(FP4X4)
-                rhs_scale = w_scales01[h][:, g, :] if h < 2 else w_scales23[:, g, DH * (h - 2) : DH * (h - 1)]
+                if h == 0:
+                    rhs_scale = w_scales0a[:, g, :] if g < 2 else w_scales0b[:, g - 2, :]
+                else:
+                    rhs_scale = w_scales[h][:, g, :]
             else:
                 rhs = wo_codes[:, h, :].bitcast(FP8X4)
                 rhs_scale = wo_scales[:, h, :]
@@ -259,7 +275,7 @@ def tile_resampler_query_projection_g5_kernel(
             c0, c1 = Q * h + P * u0, Q * h + P * u1
             nc.vector.quantize_mx(
                 out=y_codes[:, c0:c1].bitcast(FP8X4),
-                scales=y_scales[:, c0:c1],
+                scales=y_scales[h // 3][:, c0 - 3 * Q * (h // 3) : c1 - 3 * Q * (h // 3)],
                 in_=y_grp[h % 2][:, u0:u1, :].rearrange("p a c -> p (a c)"),
             )
 
@@ -270,9 +286,9 @@ def tile_resampler_query_projection_g5_kernel(
             nc.sync.dma_start(out=words_hbm[:, c0:c1], in_=y_codes[:, c0:c1].bitcast(I32))
 
         def store_scales(c0, c1, queues):
-            view = y_scales[:].bitcast(I32)
+            view = y_scales[c0 // (3 * Q)][:].bitcast(I32)
             for r in range(4):
-                queues[r].dma_start(out=scales_hbm[r][:, c0 // 4 : c1 // 4], in_=view[r:P:32, c0 // 4 : c1 // 4])
+                queues[r].dma_start(out=scales_hbm[r][:, c0 // 4 : c1 // 4], in_=view[r:P:32, :])
 
         def pair_matmuls(pair, ut):
             for g in range(2 * pair, min(2 * pair + 2, G_MAIN)):
@@ -284,20 +300,32 @@ def tile_resampler_query_projection_g5_kernel(
             for ut in range(UT):
                 x_transpose(2 * pair + ut // 2, ut % 2)
                 x_drain(2 * pair + ut // 2, ut % 2)
-            if pair > 0:
+                if pair == 0 and ut < 3:
+                    warm_pass(ut)
+            if pair == 0:
+                spread_bias()
+            else:
                 pair_matmuls(pair - 1, 3)
             for ut in range(3):
                 x_quantize(2 * pair + ut // 2, ut % 2)
                 pair_matmuls(pair, ut)
+                if pair == 3:
+                    mx_pass(1, ut, 0)
             if pair < 3:
-                x_permute(2 * pair + 2, 0, 2)
-                x_permute(2 * pair + 3, 0, 2)
+                for ut in range(UT):
+                    x_permute(2 * pair + 2 + ut // 2, ut % 2, ut % 2 + 1, ut % 2 == 0)
             x_quantize(2 * pair + 1, 1)
-        mx_pass(1, 0, 0)
-        mx_pass(1, 1, 0)
+            if pair < 2:
+                nc.vector.memset(w_scales[2 + pair][:].bitcast(I32), 0)
         pair_matmuls(3, 3)
-        mx_pass(1, 2, 0)
         mx_pass(1, 3, 0)
+
+        load_ws(w_scales[2], 1024, 1536, 0, 7)
+        load_wo(2)
+        load_w(2, 0, 7)
+        load_ws(w_scales[3], 1536, 2048, 0, 7)
+        load_wo(3)
+        load_w(3, 0, 7)
 
         def sweep(h, g0, g1):
             for g in range(g0, g1):
@@ -310,61 +338,61 @@ def tile_resampler_query_projection_g5_kernel(
         wo_group(0, 256, 512, True)
         scale_bias(2)
         wo_quantize(0)
-        sweep(1, 1, 2)
+        sweep(1, 1, 3)
         sweep(0, G_MAIN, PASSES)
-        sweep(1, 2, G_MAIN)
+        sweep(1, 3, G_MAIN)
         wo_group(1, 0, 512, False)
         for ut in range(UT):
             make_addend(0, ut)
-        for ut in range(UT):
-            finish(0, ut)
-            y_round(0, ut)
+        finish(0, 2)
+        finish(0, 3)
         wo_quantize(1)
+        finish(0, 0)
+        finish(0, 1)
         sweep(1, G_MAIN, PASSES)
-        y_transpose(0, 0, 2, 0)
-        y_transpose(0, 2, 4, 1)
-        for ut in range(UT):
-            make_addend(1, ut)
         wo_group(2, 0, 512, False)
-        y_drain(0, 0, 2, 0)
-        y_drain(0, 2, 4, 1)
-        make_addend(2, 0)
-        make_addend(2, 1)
+        for ut in range(UT):
+            y_round(0, ut)
+            make_addend(1, ut)
 
         wo_quantize(2)
         for ut in range(UT):
             finish(1, ut)
             y_round(1, ut)
-        y_quantize(0, 0, 4)
-        store_words(0, Q)
         group_matmuls(2, 0)
         group_matmuls(2, 1)
+        y_transpose(0, 0, 2, 0)
+        y_transpose(0, 2, 4, 1)
         y_transpose(1, 0, 2, 4)
         y_transpose(1, 2, 4, 5)
-        finish(2, 0)
-        y_round(2, 0)
+        for ut in range(UT):
+            make_addend(2, ut)
         scale_bias(3)
         wo_group(3, 0, 256, False)
-        make_addend(2, 2)
+        y_drain(0, 0, 2, 0)
+        y_drain(0, 2, 4, 1)
+        wo_group(3, 256, 512, False)
+        finish(2, 0)
         finish(2, 1)
-        make_addend(2, 3)
-        make_addend(3, 0)
+        y_quantize(0, 0, 4)
+        store_words(0, Q)
         y_drain(1, 0, 2, 4)
         y_drain(1, 2, 4, 5)
+        y_round(2, 0)
         y_round(2, 1)
-        wo_group(3, 256, 512, False)
-        make_addend(3, 1)
-        y_quantize(1, 0, 4)
-        store_words(Q, 2 * Q)
+        make_addend(3, 0)
+        wo_quantize(3)
         group_matmuls(2, 2)
-        make_addend(3, 2)
         finish(2, 2)
         y_round(2, 2)
-        wo_quantize(3)
-        make_addend(3, 3)
+        y_quantize(1, 0, 4)
+        store_words(Q, 2 * Q)
+        make_addend(3, 1)
+        make_addend(3, 2)
         group_matmuls(2, 3)
         finish(2, 3)
         y_round(2, 3)
+        make_addend(3, 3)
 
         group_matmuls(3, 0)
         y_transpose(2, 0, 2, 2)
@@ -383,13 +411,13 @@ def tile_resampler_query_projection_g5_kernel(
         finish(3, 2)
         y_round(3, 2)
         group_matmuls(3, 3)
-        y_transpose(3, 0, 2, 0)
-        y_transpose(3, 2, 3, 1)
+        y_transpose(3, 0, 2, 6)
+        y_transpose(3, 2, 3, 7)
         finish_bf16(3, 3)
         y_transpose(3, 3, 4, 2)
         finish(3, 3)
-        y_drain(3, 0, 2, 0)
-        y_drain(3, 2, 3, 1)
+        y_drain(3, 0, 2, 6)
+        y_drain(3, 2, 3, 7)
         y_drain(3, 3, 4, 2)
         y_quantize(3, 0, 2)
         y_quantize(3, 2, 3)

@@ -21,7 +21,7 @@ UT = Q // P
 G_MAIN = K // 512
 PASSES = G_MAIN + 1
 STEPS = 8
-WARM_PASSES = 7
+WARM_PASSES = 9
 
 
 def tile_resampler_query_projection_g5_kernel(
@@ -69,8 +69,7 @@ def tile_resampler_query_projection_g5_kernel(
         y_scales = [sb("y_scales_first", [P, 3 * Q], U8), sb("y_scales_last", [P, Q], U8)]
 
         make_identity(nc, ident[:])
-        nc.scalar.dma_start(out=bias_col[:], in_=bias.rearrange("(p j) -> p j", p=P))
-        nc.scalar.dma_start(out=hs_bf[:], in_=head_scale.partition_broadcast(P))
+        nc.gpsimd.dma_start(out=bias_col[:], in_=bias.rearrange("(p j) -> p j", p=P))
         nc.vector.memset(warm_in[:].bitcast(I32), 0)
         nc.vector.memset(w_scales0a[:].bitcast(I32), 0)
         nc.vector.quantize_mx(out=warm_codes[:].bitcast(FP8X4), scales=warm_scales[:], in_=warm_in[:])
@@ -85,7 +84,7 @@ def tile_resampler_query_projection_g5_kernel(
 
         def load_x(s):
             a0, k0 = 2 * (s % 2), 1024 * (s // 2)
-            if s < 2:
+            if s < 1:
                 for a in range(2):
                     nc.sync.dma_start(out=x_raw[s][:, a, :], in_=x_hbm[:, a0 + a, 0:1024])
             elif k0 + 1024 <= K:
@@ -121,11 +120,11 @@ def tile_resampler_query_projection_g5_kernel(
         load_ws(w_scales[1], 512, 1024, 0, 7)
         load_w(1, 0, 3)
         load_wo(0)
+        nc.sync.dma_start(out=hs_bf[:], in_=head_scale.partition_broadcast(P))
         load_w(1, 3, 7)
         nc.sync.dma_start(out=pos_sb[:], in_=pos.rearrange("(a p) d -> p a d", p=P))
         load_wo(1)
 
-        nc.vector.tensor_copy(out=hs[:], in_=hs_bf[:])
 
         def warm_pass(q):
             nc.tensor.matmul_mx(
@@ -305,24 +304,30 @@ def tile_resampler_query_projection_g5_kernel(
             if pair == 0:
                 spread_bias()
             else:
+                pair_matmuls(pair - 1, 2)
                 pair_matmuls(pair - 1, 3)
-            for ut in range(3):
-                x_quantize(2 * pair + ut // 2, ut % 2)
+            for ut in range(2):
+                x_quantize(2 * pair, ut)
                 pair_matmuls(pair, ut)
                 if pair == 3:
                     mx_pass(1, ut, 0)
             if pair < 3:
-                for ut in range(UT):
-                    x_permute(2 * pair + 2 + ut // 2, ut % 2, ut % 2 + 1, ut % 2 == 0)
+                x_permute(2 * pair + 2, 0, 2)
+            x_quantize(2 * pair + 1, 0)
+            if pair < 3:
+                x_permute(2 * pair + 3, 0, 1)
+                x_permute(2 * pair + 3, 1, 2, False)
             x_quantize(2 * pair + 1, 1)
             if pair < 2:
                 nc.vector.memset(w_scales[2 + pair][:].bitcast(I32), 0)
-        pair_matmuls(3, 3)
-        mx_pass(1, 3, 0)
+        for ut in range(2, UT):
+            pair_matmuls(3, ut)
+            mx_pass(1, ut, 0)
 
         load_ws(w_scales[2], 1024, 1536, 0, 7)
         load_wo(2)
-        load_w(2, 0, 7)
+        load_w(2, 0, 3)
+        load_w(2, 3, 7)
         load_ws(w_scales[3], 1536, 2048, 0, 7)
         load_wo(3)
         load_w(3, 0, 7)
@@ -332,12 +337,13 @@ def tile_resampler_query_projection_g5_kernel(
                 for ut in range(UT):
                     mx_pass(h, ut, g)
 
-        scale_bias(0)
-        scale_bias(1)
         wo_group(0, 0, 256, False)
         wo_group(0, 256, 512, True)
-        scale_bias(2)
+        nc.vector.tensor_copy(out=hs[:], in_=hs_bf[:])
         wo_quantize(0)
+        scale_bias(0)
+        scale_bias(1)
+        scale_bias(2)
         sweep(1, 1, 3)
         sweep(0, G_MAIN, PASSES)
         sweep(1, 3, G_MAIN)

@@ -17,11 +17,18 @@ MULT = mybir.AluOpType.mult
 ADD = mybir.AluOpType.add
 
 P = 128
-UT = Q // P
-G_MAIN = K // 512
-PASSES = G_MAIN + 1
-STEPS = 8
-WARM_PASSES = 9
+TILES = Q // P
+K_PASS = 4 * P
+MAIN_PASSES = K // K_PASS
+PASSES = MAIN_PASSES + 1
+PAIRS = PASSES // 2
+SCALE_ROWS = 4
+FIRST_PASSES = 2
+WARM_PASSES = 10
+
+GROUP_BANK = [[0, 1, 2, 3], [4, 5, 6, 7], [2, 3, 6, 7], [0, 1, 4, 5]]
+X_BANK = 4
+SPARE_BANK = 2
 
 
 def tile_resampler_query_projection_g5_kernel(
@@ -40,394 +47,388 @@ def tile_resampler_query_projection_g5_kernel(
 
         ident = sb("ident", [P, P], F32)
         bias_col = sb("bias_col", [P, 16], BF16)
-        hs_bf = sb("hs_bf", [P, H], BF16)
-        hs = sb("hs", [P, H], F32)
+        scale_bf = sb("scale_bf", [P, H], BF16)
+        scale = sb("scale", [P, H], F32)
         warm_in = sb("warm_in", [P, 8 * P], BF16)
         warm_codes = sb("warm_codes", [P, 2 * P], U32)
         warm_scales = sb("warm_scales", [P, 2 * P], U8)
-        bias_bc = sb("bias_bc", [P, H, DH], BF16)
-        bias_hs = sb("bias_hs", [P, H, DH], F32)
-        pos_sb = sb("pos_sb", [P, UT, DH], BF16)
-        x_raw = [sb("x_raw%d" % s, [P, 2, 1024], BF16) for s in range(STEPS)]
-        x_perm = [sb("x_perm%d" % i, [P, 4, 2, P], F32) for i in range(2)]
-        x_grp = [sb("x_grp%d" % i, [P, 2, 1024], BF16) for i in range(2)]
-        x_codes = sb("x_codes", [P, UT, PASSES * P], U32)
-        x_scales = sb("x_scales", [P, UT, PASSES * P], U8)
-        w_words = [sb("w_words%d" % h, [P, G_MAIN, 2 * DH], U8) for h in range(H)]
-        w_scales0a = sb("w_scales0a", [P, 2, DH], U8)
-        w_scales0b = sb("w_scales0b", [P, G_MAIN - 2, DH], U8)
-        w_scales = [None] + [sb("w_scales%d" % h, [P, G_MAIN, DH], U8) for h in range(1, H)]
+        bias_all = sb("bias_all", [P, H, DH], BF16)
+        bias_scaled = sb("bias_scaled", [P, H, DH], F32)
+        pos_sb = sb("pos_sb", [P, TILES, DH], BF16)
+        x_raw = [sb("x_raw%d" % c, [P, 2, 2 * K_PASS], BF16) for c in range(2 * PAIRS)]
+        x_halves = [sb("x_halves%d" % i, [P, 4, 2, P], F32) for i in range(2)]
+        x_turned = [sb("x_turned%d" % i, [P, 2, 2 * K_PASS], BF16) for i in range(2)]
+        x_codes = sb("x_codes", [P, TILES, PASSES * P], U32)
+        x_scales = sb("x_scales", [P, TILES, PASSES * P], U8)
+        w_codes = [sb("w_codes%d" % h, [P, MAIN_PASSES, 2 * DH], U8) for h in range(H)]
+        w_scales_first = sb("w_scales_first", [P, FIRST_PASSES, DH], U8)
+        w_scales = [sb("w_scales0", [P, MAIN_PASSES - FIRST_PASSES, DH], U8)]
+        w_scales += [sb("w_scales%d" % h, [P, MAIN_PASSES, DH], U8) for h in range(1, H)]
         wo_raw = [sb("wo_raw%d" % h, [P, 4, DH], BF16) for h in range(H)]
-        wo_grp = [sb("wo_grp%d" % i, [P, DH, 4], BF16) for i in range(2)]
+        wo_grouped = [sb("wo_grouped%d" % i, [P, DH, 4], BF16) for i in range(2)]
         wo_codes = sb("wo_codes", [P, H, DH], U32)
         wo_scales = sb("wo_scales", [P, H, DH], U8)
-        addend = [sb("addend%d" % i, [P, UT, DH], F32) for i in range(2)]
-        y = [sb("y%d" % h, [P, UT, DH], F32) for h in range(3)]
-        y_bf = [sb("y_bf%d" % i, [P, UT, 2, P, 2], BF16) for i in range(2)]
-        y_grp = [sb("y_grp%d" % i, [P, UT, DH], BF16) for i in range(2)]
+        addend = [sb("addend%d" % i, [P, TILES, DH], F32) for i in range(2)]
+        y = [sb("y%d" % i, [P, TILES, DH], F32) for i in range(3)]
+        y_halves = [sb("y_halves%d" % i, [P, TILES, 2, P, 2], BF16) for i in range(3)]
+        y_turned = [sb("y_turned%d" % i, [P, TILES, DH], BF16) for i in range(2)]
         y_codes = sb("y_codes", [P, H * Q], U32)
-        y_scales = [sb("y_scales_first", [P, 3 * Q], U8), sb("y_scales_last", [P, Q], U8)]
-
-        make_identity(nc, ident[:])
-        nc.gpsimd.dma_start(out=bias_col[:], in_=bias.rearrange("(p j) -> p j", p=P))
-        nc.vector.memset(warm_in[:].bitcast(I32), 0)
-        nc.vector.memset(w_scales0a[:].bitcast(I32), 0)
-        nc.vector.quantize_mx(out=warm_codes[:].bitcast(FP8X4), scales=warm_scales[:], in_=warm_in[:])
-        nc.vector.memset(w_scales0b[:].bitcast(I32), 0)
-        nc.vector.memset(w_scales[1][:].bitcast(I32), 0)
+        y_scales = [sb("y_scales_first", [P, (H - 1) * Q], U8), sb("y_scales_last", [P, Q], U8)]
 
         x_hbm = queries.rearrange("(a p) k -> p a k", p=P)
         xo_hbm = queries_outlier.rearrange("(a p) k -> p a k", p=P)
-        ww_hbm = wq_words.bitcast(I32).rearrange("g p c -> p g c")
-        ws_hbm = wq_scales.bitcast(I32).rearrange("g (q r) c -> r q g c", r=4)
-        wo_hbm = w_outlier.rearrange("(p j) c -> p j c", j=4)
+        w_codes_hbm = wq_words.bitcast(I32).rearrange("g p c -> p g c")
+        w_scales_hbm = wq_scales.bitcast(I32).rearrange("g (q r) c -> r q g c", r=SCALE_ROWS)
+        wo_hbm = w_outlier.rearrange("(p t) c -> p t c", t=4)
+        y_codes_hbm = out_1[0].rearrange("p m t -> p (m t)").bitcast(I32)
+        y_scales_hbm = out_2[0].bitcast(I32).rearrange("(q r) c -> r q c", r=SCALE_ROWS)
 
-        def load_x(s):
-            a0, k0 = 2 * (s % 2), 1024 * (s // 2)
-            if s < 1:
-                for a in range(2):
-                    nc.sync.dma_start(out=x_raw[s][:, a, :], in_=x_hbm[:, a0 + a, 0:1024])
-            elif k0 + 1024 <= K:
-                nc.sync.dma_start(out=x_raw[s][:], in_=x_hbm[:, a0 : a0 + 2, k0 : k0 + 1024])
-            else:
-                nc.sync.dma_start(out=x_raw[s][:, :, 0:512], in_=x_hbm[:, a0 : a0 + 2, k0:K])
-                nc.sync.dma_start(out=x_raw[s][:, :, 512:1024], in_=xo_hbm[:, a0 : a0 + 2, :])
+        def load_x(pair):
+            k0 = 2 * K_PASS * pair
+            for half in range(2):
+                dst = x_raw[2 * pair + half]
+                tiles = slice(2 * half, 2 * half + 2)
+                if pair == 0:
+                    for a in range(2):
+                        nc.sync.dma_start(out=dst[:, a, :], in_=x_hbm[:, 2 * half + a, 0 : 2 * K_PASS])
+                elif pair < PAIRS - 1:
+                    nc.sync.dma_start(out=dst[:], in_=x_hbm[:, tiles, k0 : k0 + 2 * K_PASS])
+                else:
+                    nc.sync.dma_start(out=dst[:, :, 0:K_PASS], in_=x_hbm[:, tiles, k0:K])
+                    nc.sync.dma_start(out=dst[:, :, K_PASS : 2 * K_PASS], in_=xo_hbm[:, tiles, :])
 
-        def load_w(h, g0, g1):
-            nc.sync.dma_start(out=w_words[h][:].bitcast(I32)[:, g0:g1, :], in_=ww_hbm[:, g0:g1, 256 * h : 256 * (h + 1)])
+        def load_w_codes(h, g0, g1):
+            cols = slice(DH // 2 * h, DH // 2 * (h + 1))
+            nc.sync.dma_start(out=w_codes[h][:].bitcast(I32)[:, g0:g1, :], in_=w_codes_hbm[:, g0:g1, cols])
 
-        def load_ws(tile, c0, c1, g0, g1):
-            view = tile[:].bitcast(I32)
-            for r in range(4):
-                nc.sync.dma_start(out=view[r:P:32, :, :], in_=ws_hbm[r][:, g0:g1, c0 // 4 : c1 // 4])
+        def load_w_scales(dst, h, g0, g1):
+            cols = slice(DH // 4 * h, DH // 4 * (h + 1))
+            for r in range(SCALE_ROWS):
+                nc.sync.dma_start(out=dst[:].bitcast(I32)[r:P:32, :, :], in_=w_scales_hbm[r][:, g0:g1, cols])
 
         def load_wo(h):
             nc.sync.dma_start(out=wo_raw[h][:], in_=wo_hbm[:, :, DH * h : DH * (h + 1)])
 
-        load_x(0)
-        load_x(1)
-        load_ws(w_scales0a, 0, 512, 0, 2)
-        load_w(0, 0, 2)
-        load_x(2)
-        load_x(3)
-        load_ws(w_scales0b, 0, 512, 2, 7)
-        load_w(0, 2, 4)
-        load_x(4)
-        load_x(5)
-        load_w(0, 4, 7)
-        load_x(6)
-        load_x(7)
-        load_ws(w_scales[1], 512, 1024, 0, 7)
-        load_w(1, 0, 3)
-        load_wo(0)
-        nc.sync.dma_start(out=hs_bf[:], in_=head_scale.partition_broadcast(P))
-        load_w(1, 3, 7)
-        nc.sync.dma_start(out=pos_sb[:], in_=pos.rearrange("(a p) d -> p a d", p=P))
-        load_wo(1)
+        def clear(scale_tile):
+            nc.vector.memset(scale_tile[:].bitcast(I32), 0)
 
-
-        def warm_pass(q):
-            nc.tensor.matmul_mx(
-                out=bank[2 + q // 2 % 2][:, 2 * P * (q % 2) : 2 * P * (q % 2 + 1)],
-                lhsT=warm_codes[:, 0:P].bitcast(FP8X4), lhsT_scale=warm_scales[:, 0:P],
-                rhs=warm_codes[:].bitcast(FP8X4), rhs_scale=warm_scales[:],
-                start=True, stop=True,
-            )
-
-        for q in range(WARM_PASSES):
-            warm_pass(q)
-
-        def spread_bias():
-            bias_words = bias_col[:].bitcast(F32)
-            bias_bc_words = bias_bc[:].rearrange("p h d -> p (h d)").bitcast(F32).rearrange("p (n j) -> p n j", j=8)
-            for b in range(2):
-                for q in range(4):
-                    j = 4 * b + q
-                    nc.tensor.transpose(
-                        bank[2 + b][:, P * q : P * (q + 1)], bias_words[:, j : j + 1].to_broadcast([P, P]), ident[:]
-                    )
-                nc.scalar.copy(
-                    out=bias_bc_words[:, :, 4 * b : 4 * b + 4], in_=bank[2 + b][:].rearrange("p (j n) -> p n j", j=4)
-                )
-
-        def x_permute(s, a0, a1, on_vector=True):
-            words = x_raw[s][:, a0:a1, :].bitcast(F32).rearrange("p a (g w j) -> p (a g) j w", g=2, j=2)
-            if on_vector:
-                nc.vector.tensor_copy(out=x_perm[s % 2][:, 2 * a0 : 2 * a1, :, :], in_=words)
-            else:
-                nc.scalar.copy(out=x_perm[s % 2][:, 2 * a0 : 2 * a1, :, :], in_=words)
-
-        def x_transpose(s, a):
-            dst = bank[4 + 2 * (s % 2) + a]
-            for g in range(2):
-                for j in range(2):
-                    q = 2 * g + j
-                    nc.tensor.transpose(dst[:, P * q : P * (q + 1)], x_perm[s % 2][:, 2 * a + g, j, :], ident[:])
-
-        def x_drain(s, a):
-            nc.scalar.copy(
-                out=x_grp[s % 2][:, a, :].bitcast(F32).rearrange("p (g u j) -> p g u j", g=2, j=2),
-                in_=bank[4 + 2 * (s % 2) + a][:].rearrange("p (g j u) -> p g u j", g=2, j=2),
-            )
-
-        def x_quantize(s, a):
-            ut, c0 = 2 * (s % 2) + a, 2 * P * (s // 2)
-            nc.vector.quantize_mx(
-                out=x_codes[:, ut, c0 : c0 + 2 * P].bitcast(FP8X4),
-                scales=x_scales[:, ut, c0 : c0 + 2 * P],
-                in_=x_grp[s % 2][:, a, :],
-            )
-
-        def wo_group(h, c0, c1, on_vector):
-            dst = wo_grp[h % 2][:, c0:c1, :]
-            src = wo_raw[h][:, :, c0:c1].rearrange("p j c -> p c j")
+        def copy(on_vector, dst, src):
             if on_vector:
                 nc.vector.tensor_copy(out=dst, in_=src)
             else:
                 nc.scalar.copy(out=dst, in_=src)
 
+        def warm_pass(i):
+            nc.tensor.matmul_mx(
+                out=bank[SPARE_BANK + i // 2 % 2][:, 2 * P * (i % 2) : 2 * P * (i % 2 + 1)],
+                lhsT=warm_codes[:, 0:P].bitcast(FP8X4),
+                lhsT_scale=warm_scales[:, 0:P],
+                rhs=warm_codes[:].bitcast(FP8X4),
+                rhs_scale=warm_scales[:],
+                start=True,
+                stop=True,
+            )
+
+        def spread_bias():
+            words = bias_col[:].bitcast(F32)
+            dst = bias_all[:].rearrange("p h d -> p (h d)").bitcast(F32).rearrange("p (n j) -> p n j", j=8)
+            for b in range(2):
+                spare = bank[SPARE_BANK + b]
+                for q in range(4):
+                    j = 4 * b + q
+                    nc.tensor.transpose(
+                        spare[:, P * q : P * (q + 1)], words[:, j : j + 1].to_broadcast([P, P]), ident[:]
+                    )
+                nc.scalar.copy(out=dst[:, :, 4 * b : 4 * b + 4], in_=spare[:].rearrange("p (j n) -> p n j", j=4))
+
+        def x_split(pair, tile, on_vector):
+            a = tile % 2
+            words = x_raw[2 * pair + tile // 2][:, a : a + 1, :].bitcast(F32)
+            src = words.rearrange("p a (g w j) -> p (a g) j w", g=2, j=2)
+            copy(on_vector, x_halves[tile // 2][:, 2 * a : 2 * a + 2, :, :], src)
+
+        def x_turn(tile):
+            a, dst = tile % 2, bank[X_BANK + tile]
+            for g in range(2):
+                for j in range(2):
+                    q = 2 * g + j
+                    nc.tensor.transpose(dst[:, P * q : P * (q + 1)], x_halves[tile // 2][:, 2 * a + g, j, :], ident[:])
+            nc.scalar.copy(
+                out=x_turned[tile // 2][:, a, :].bitcast(F32).rearrange("p (g u j) -> p g u j", g=2, j=2),
+                in_=dst[:].rearrange("p (g j u) -> p g u j", g=2, j=2),
+            )
+
+        def x_quantize(pair, tile):
+            cols = slice(2 * P * pair, 2 * P * (pair + 1))
+            nc.vector.quantize_mx(
+                out=x_codes[:, tile, cols].bitcast(FP8X4),
+                scales=x_scales[:, tile, cols],
+                in_=x_turned[tile // 2][:, tile % 2, :],
+            )
+
+        def wo_group(h, c0, c1, on_vector):
+            copy(on_vector, wo_grouped[h % 2][:, c0:c1, :], wo_raw[h][:, :, c0:c1].rearrange("p t c -> p c t"))
+
         def wo_quantize(h):
             nc.vector.quantize_mx(
                 out=wo_codes[:, h, :].bitcast(FP8X4),
                 scales=wo_scales[:, h, :],
-                in_=wo_grp[h % 2][:].rearrange("p c j -> p (c j)"),
+                in_=wo_grouped[h % 2][:].rearrange("p c t -> p (c t)"),
             )
 
-        acc_bank = [[0, 1, 2, 3], [4, 5, 6, 7], [2, 3, 6, 7], [0, 1, 4, 5]]
-
-        def mx_pass(h, ut, g):
-            if g < G_MAIN:
-                rhs = w_words[h][:, g, :].bitcast(FP4X4)
-                if h == 0:
-                    rhs_scale = w_scales0a[:, g, :] if g < 2 else w_scales0b[:, g - 2, :]
-                else:
-                    rhs_scale = w_scales[h][:, g, :]
+        def mx_pass(h, tile, g):
+            if g == MAIN_PASSES:
+                rhs, rhs_scale = wo_codes[:, h, :].bitcast(FP8X4), wo_scales[:, h, :]
             else:
-                rhs = wo_codes[:, h, :].bitcast(FP8X4)
-                rhs_scale = wo_scales[:, h, :]
+                rhs = w_codes[h][:, g, :].bitcast(FP4X4)
+                if h > 0:
+                    rhs_scale = w_scales[h][:, g, :]
+                elif g < FIRST_PASSES:
+                    rhs_scale = w_scales_first[:, g, :]
+                else:
+                    rhs_scale = w_scales[0][:, g - FIRST_PASSES, :]
             nc.tensor.matmul_mx(
-                out=bank[acc_bank[h][ut]][:],
-                lhsT=x_codes[:, ut, P * g : P * (g + 1)].bitcast(FP8X4),
-                lhsT_scale=x_scales[:, ut, P * g : P * (g + 1)],
+                out=bank[GROUP_BANK[h][tile]][:],
+                lhsT=x_codes[:, tile, P * g : P * (g + 1)].bitcast(FP8X4),
+                lhsT_scale=x_scales[:, tile, P * g : P * (g + 1)],
                 rhs=rhs,
                 rhs_scale=rhs_scale,
                 start=(g == 0),
                 stop=(g == PASSES - 1),
             )
 
-        def step_matmuls(s):
-            for g in range(2 * (s // 2), 2 * (s // 2) + 2):
-                for a in range(2):
-                    mx_pass(0, 2 * (s % 2) + a, g)
-
-        def group_matmuls(h, ut):
-            for g in range(PASSES):
-                mx_pass(h, ut, g)
-
-        def scale_bias(h):
-            nc.vector.tensor_scalar(
-                out=bias_hs[:, h, :], in0=bias_bc[:, h, :], scalar1=hs[:, h : h + 1], scalar2=None, op0=MULT
-            )
-
-        def make_addend(h, ut):
-            nc.vector.scalar_tensor_tensor(
-                out=addend[h % 2][:, ut, :], in0=pos_sb[:, ut, :], scalar=hs[:, h : h + 1], in1=bias_hs[:, h, :],
-                op0=MULT, op1=ADD,
-            )
-
-        def finish(h, ut):
-            nc.vector.scalar_tensor_tensor(
-                out=y[h % 3][:, ut, :], in0=bank[acc_bank[h][ut]][:], scalar=hs[:, h : h + 1], in1=addend[h % 2][:, ut, :],
-                op0=MULT, op1=ADD,
-            )
-            nc.sync.dma_start(out=out_0[h, P * ut : P * (ut + 1), :], in_=y[h % 3][:, ut, :])
-
-        def finish_bf16(h, ut):
-            acc = bank[acc_bank[h][ut]][:].rearrange("p (w j e) -> p j w e", j=2, e=2)
-            add = addend[h % 2][:, ut, :].rearrange("p (w j e) -> p j w e", j=2, e=2)
-            for j in range(2):
-                nc.vector.scalar_tensor_tensor(
-                    out=y_bf[h % 2][:, ut, j, :, :], in0=acc[:, j, :, :], scalar=hs[:, h : h + 1], in1=add[:, j, :, :],
-                    op0=MULT, op1=ADD,
-                )
-
-        def y_round(h, ut):
-            nc.scalar.copy(
-                out=y_bf[h % 2][:, ut, :, :, :], in_=y[h % 3][:, ut, :].rearrange("p (w j e) -> p j w e", j=2, e=2)
-            )
-
-        def y_transpose(h, u0, u1, b):
-            for ut in range(u0, u1):
-                for j in range(2):
-                    q = 2 * (ut - u0) + j
-                    words = y_bf[h % 2][:, ut, j, :, :].rearrange("p w e -> p (w e)").bitcast(F32)
-                    nc.tensor.transpose(bank[b][:, P * q : P * (q + 1)], words, ident[:])
-
-        def y_drain(h, u0, u1, b):
-            n = u1 - u0
-            nc.scalar.copy(
-                out=y_grp[h % 2][:, u0:u1, :].bitcast(F32).rearrange("p a (u j) -> p a u j", j=2),
-                in_=bank[b][:, 0 : 2 * P * n].rearrange("p (a j u) -> p a u j", a=n, j=2),
-            )
-
-        def y_quantize(h, u0, u1):
-            c0, c1 = Q * h + P * u0, Q * h + P * u1
-            nc.vector.quantize_mx(
-                out=y_codes[:, c0:c1].bitcast(FP8X4),
-                scales=y_scales[h // 3][:, c0 - 3 * Q * (h // 3) : c1 - 3 * Q * (h // 3)],
-                in_=y_grp[h % 2][:, u0:u1, :].rearrange("p a c -> p (a c)"),
-            )
-
-        words_hbm = out_1[0].rearrange("p m t -> p (m t)").bitcast(I32)
-        scales_hbm = out_2[0].bitcast(I32).rearrange("(q r) c -> r q c", r=4)
-
-        def store_words(c0, c1):
-            nc.sync.dma_start(out=words_hbm[:, c0:c1], in_=y_codes[:, c0:c1].bitcast(I32))
-
-        def store_scales(c0, c1, queues):
-            view = y_scales[c0 // (3 * Q)][:].bitcast(I32)
-            for r in range(4):
-                queues[r].dma_start(out=scales_hbm[r][:, c0 // 4 : c1 // 4], in_=view[r:P:32, :])
-
-        def pair_matmuls(pair, ut):
-            for g in range(2 * pair, min(2 * pair + 2, G_MAIN)):
-                mx_pass(0, ut, g)
-
-        for ut in range(UT):
-            x_permute(ut // 2, ut % 2, ut % 2 + 1)
-        for pair in range(4):
-            for ut in range(UT):
-                x_transpose(2 * pair + ut // 2, ut % 2)
-                x_drain(2 * pair + ut // 2, ut % 2)
-                if pair == 0 and ut < 3:
-                    warm_pass(ut)
-            if pair == 0:
-                spread_bias()
-            else:
-                pair_matmuls(pair - 1, 2)
-                pair_matmuls(pair - 1, 3)
-            for ut in range(2):
-                x_quantize(2 * pair, ut)
-                pair_matmuls(pair, ut)
-                if pair == 3:
-                    mx_pass(1, ut, 0)
-            if pair < 3:
-                x_permute(2 * pair + 2, 0, 2)
-            x_quantize(2 * pair + 1, 0)
-            if pair < 3:
-                x_permute(2 * pair + 3, 0, 1)
-                x_permute(2 * pair + 3, 1, 2, False)
-            x_quantize(2 * pair + 1, 1)
-            if pair < 2:
-                nc.vector.memset(w_scales[2 + pair][:].bitcast(I32), 0)
-        for ut in range(2, UT):
-            pair_matmuls(3, ut)
-            mx_pass(1, ut, 0)
-
-        load_ws(w_scales[2], 1024, 1536, 0, 7)
-        load_wo(2)
-        load_w(2, 0, 3)
-        load_w(2, 3, 7)
-        load_ws(w_scales[3], 1536, 2048, 0, 7)
-        load_wo(3)
-        load_w(3, 0, 7)
+        def head0_pair(pair, tile):
+            for g in range(2 * pair, min(2 * pair + 2, MAIN_PASSES)):
+                mx_pass(0, tile, g)
 
         def sweep(h, g0, g1):
             for g in range(g0, g1):
-                for ut in range(UT):
-                    mx_pass(h, ut, g)
+                for tile in range(TILES):
+                    mx_pass(h, tile, g)
 
-        wo_group(0, 0, 256, False)
-        wo_group(0, 256, 512, True)
-        nc.vector.tensor_copy(out=hs[:], in_=hs_bf[:])
+        def group(h, tile):
+            for g in range(PASSES):
+                mx_pass(h, tile, g)
+
+        def scale_bias(h):
+            nc.vector.tensor_scalar(
+                out=bias_scaled[:, h, :], in0=bias_all[:, h, :], scalar1=scale[:, h : h + 1], scalar2=None, op0=MULT
+            )
+
+        def multiply_add(h, dst, in0, in1):
+            nc.vector.scalar_tensor_tensor(out=dst, in0=in0, scalar=scale[:, h : h + 1], in1=in1, op0=MULT, op1=ADD)
+
+        def make_addend(h, *tiles):
+            for tile in tiles:
+                multiply_add(h, addend[h % 2][:, tile, :], pos_sb[:, tile, :], bias_scaled[:, h, :])
+
+        def finish(h, *tiles):
+            for tile in tiles:
+                dst = y[h % 3][:, tile, :]
+                multiply_add(h, dst, bank[GROUP_BANK[h][tile]][:], addend[h % 2][:, tile, :])
+                nc.sync.dma_start(out=out_0[h, P * tile : P * (tile + 1), :], in_=dst)
+
+        def by_halves(ap):
+            return ap.rearrange("p (w j e) -> p j w e", j=2, e=2)
+
+        def y_round(h, *tiles):
+            for tile in tiles:
+                nc.scalar.copy(out=y_halves[h % 3][:, tile, :, :, :], in_=by_halves(y[h % 3][:, tile, :]))
+
+        def y_round_from_psum(h, tile):
+            sums, add = by_halves(bank[GROUP_BANK[h][tile]][:]), by_halves(addend[h % 2][:, tile, :])
+            for j in range(2):
+                multiply_add(h, y_halves[h % 3][:, tile, j, :, :], sums[:, j, :, :], add[:, j, :, :])
+
+        def y_turn(h, t0, t1, b):
+            for tile in range(t0, t1):
+                for j in range(2):
+                    q = 2 * (tile - t0) + j
+                    words = y_halves[h % 3][:, tile, j, :, :].rearrange("p w e -> p (w e)").bitcast(F32)
+                    nc.tensor.transpose(bank[b][:, P * q : P * (q + 1)], words, ident[:])
+
+        def y_drain(h, t0, t1, b):
+            nc.scalar.copy(
+                out=y_turned[h % 2][:, t0:t1, :].bitcast(F32).rearrange("p a (u j) -> p a u j", j=2),
+                in_=bank[b][:, 0 : 2 * P * (t1 - t0)].rearrange("p (a j u) -> p a u j", a=t1 - t0, j=2),
+            )
+
+        def y_quantize(h, t0, t1):
+            last = h // (H - 1)
+            c0, c1, base = Q * h + P * t0, Q * h + P * t1, (H - 1) * Q * last
+            nc.vector.quantize_mx(
+                out=y_codes[:, c0:c1].bitcast(FP8X4),
+                scales=y_scales[last][:, c0 - base : c1 - base],
+                in_=y_turned[h % 2][:, t0:t1, :].rearrange("p a c -> p (a c)"),
+            )
+
+        def store_codes(h, t0, t1):
+            cols = slice(Q * h + P * t0, Q * h + P * t1)
+            nc.sync.dma_start(out=y_codes_hbm[:, cols], in_=y_codes[:, cols].bitcast(I32))
+
+        def store_scales(last, h0, h1, queues):
+            cols = slice(Q // 4 * h0, Q // 4 * h1)
+            for r in range(SCALE_ROWS):
+                queues[r].dma_start(out=y_scales_hbm[r][:, cols], in_=y_scales[last][:].bitcast(I32)[r:P:32, :])
+
+        def head_banks(h):
+            return [(0, 2, [0, 4, 2][h]), (2, 4, [1, 5, 3][h])]
+
+        def turn_head(h):
+            for t0, t1, b in head_banks(h):
+                y_turn(h, t0, t1, b)
+
+        def drain_head(h):
+            for t0, t1, b in head_banks(h):
+                y_drain(h, t0, t1, b)
+
+        def quantize_head(h):
+            y_quantize(h, 0, TILES)
+            store_codes(h, 0, TILES)
+
+        make_identity(nc, ident[:])
+        nc.gpsimd.dma_start(out=bias_col[:], in_=bias.rearrange("(p j) -> p j", p=P))
+        nc.vector.memset(warm_in[:].bitcast(I32), 0)
+        clear(w_scales_first)
+        nc.vector.quantize_mx(out=warm_codes[:].bitcast(FP8X4), scales=warm_scales[:], in_=warm_in[:])
+        clear(w_scales[0])
+        clear(w_scales[1])
+
+        load_x(0)
+        load_w_scales(w_scales_first, 0, 0, FIRST_PASSES)
+        load_w_codes(0, 0, 2)
+        load_x(1)
+        load_w_scales(w_scales[0], 0, FIRST_PASSES, MAIN_PASSES)
+        load_w_codes(0, 2, 4)
+        load_x(2)
+        load_w_codes(0, 4, MAIN_PASSES)
+        load_x(3)
+        load_w_scales(w_scales[1], 1, 0, MAIN_PASSES)
+        load_w_codes(1, 0, 3)
+        nc.sync.dma_start(out=scale_bf[:], in_=head_scale.partition_broadcast(P))
+        load_wo(0)
+        nc.sync.dma_start(out=pos_sb[:], in_=pos.rearrange("(a p) d -> p a d", p=P))
+        load_w_codes(1, 3, MAIN_PASSES)
+        load_wo(1)
+
+        for i in range(WARM_PASSES):
+            warm_pass(i)
+
+        for tile in range(TILES):
+            x_split(0, tile, True)
+        for pair in range(PAIRS):
+            first, last = pair == 0, pair == PAIRS - 1
+            for tile in range(TILES):
+                x_turn(tile)
+                if first and tile < 2:
+                    warm_pass(tile)
+            if first:
+                spread_bias()
+            else:
+                head0_pair(pair - 1, 2)
+                head0_pair(pair - 1, 3)
+            for tile in range(2):
+                x_quantize(pair, tile)
+                head0_pair(pair, tile)
+                if last:
+                    mx_pass(1, tile, 0)
+            if not last:
+                for tile in range(3):
+                    x_split(pair + 1, tile, True)
+            x_quantize(pair, 2)
+            if not last:
+                x_split(pair + 1, 3, False)
+            x_quantize(pair, 3)
+            if pair < 2:
+                clear(w_scales[2 + pair])
+        for tile in range(2, TILES):
+            head0_pair(PAIRS - 1, tile)
+            mx_pass(1, tile, 0)
+
+        load_w_scales(w_scales[2], 2, 0, MAIN_PASSES)
+        load_wo(2)
+        load_w_codes(2, 0, 3)
+        load_w_codes(2, 3, MAIN_PASSES)
+        load_w_scales(w_scales[3], 3, 0, MAIN_PASSES)
+        load_wo(3)
+        load_w_codes(3, 0, MAIN_PASSES)
+
+
+        nc.vector.tensor_copy(out=scale[:], in_=scale_bf[:])
+        for h in range(H - 1):
+            scale_bias(h)
+        wo_group(0, 0, DH // 2, False)
+        wo_group(0, DH // 2, DH, True)
+        make_addend(0, 2)
         wo_quantize(0)
-        scale_bias(0)
-        scale_bias(1)
-        scale_bias(2)
-        sweep(1, 1, 3)
-        sweep(0, G_MAIN, PASSES)
-        sweep(1, 3, G_MAIN)
-        wo_group(1, 0, 512, False)
-        for ut in range(UT):
-            make_addend(0, ut)
-        finish(0, 2)
-        finish(0, 3)
+        make_addend(0, 3, 0, 1)
+        sweep(1, 1, 4)
+        sweep(0, MAIN_PASSES, PASSES)
+        sweep(1, 4, MAIN_PASSES)
+        wo_group(1, 0, DH, False)
+        finish(0, 2, 3)
+        make_addend(1, 0)
         wo_quantize(1)
-        finish(0, 0)
-        finish(0, 1)
-        sweep(1, G_MAIN, PASSES)
-        wo_group(2, 0, 512, False)
-        for ut in range(UT):
-            y_round(0, ut)
-            make_addend(1, ut)
-
+        finish(0, 0, 1)
+        sweep(1, MAIN_PASSES, PASSES)
+        wo_group(2, 0, DH, False)
+        y_round(0, 0, 1)
+        make_addend(1, 1, 2)
         wo_quantize(2)
-        for ut in range(UT):
-            finish(1, ut)
-            y_round(1, ut)
-        group_matmuls(2, 0)
-        group_matmuls(2, 1)
-        y_transpose(0, 0, 2, 0)
-        y_transpose(0, 2, 4, 1)
-        y_transpose(1, 0, 2, 4)
-        y_transpose(1, 2, 4, 5)
-        for ut in range(UT):
-            make_addend(2, ut)
+        y_round(0, 2, 3)
+        make_addend(1, 3)
+
+        finish(1, 2, 3, 0, 1)
+        y_round(1, 0, 1, 2, 3)
+        for tile in range(3):
+            group(2, tile)
+        turn_head(0)
+        turn_head(1)
+        make_addend(2, 0, 1)
+        finish(2, 0, 1)
+        make_addend(2, 2)
         scale_bias(3)
-        wo_group(3, 0, 256, False)
-        y_drain(0, 0, 2, 0)
-        y_drain(0, 2, 4, 1)
-        wo_group(3, 256, 512, False)
-        finish(2, 0)
-        finish(2, 1)
-        y_quantize(0, 0, 4)
-        store_words(0, Q)
-        y_drain(1, 0, 2, 4)
-        y_drain(1, 2, 4, 5)
-        y_round(2, 0)
-        y_round(2, 1)
+        wo_group(3, 0, DH, False)
+        make_addend(2, 3)
+        finish(2, 2)
+        drain_head(0)
+        drain_head(1)
         make_addend(3, 0)
         wo_quantize(3)
-        group_matmuls(2, 2)
-        finish(2, 2)
-        y_round(2, 2)
-        y_quantize(1, 0, 4)
-        store_words(Q, 2 * Q)
+        group(2, 3)
         make_addend(3, 1)
-        make_addend(3, 2)
-        group_matmuls(2, 3)
+        quantize_head(0)
         finish(2, 3)
-        y_round(2, 3)
-        make_addend(3, 3)
+        y_round(2, 0, 1, 2, 3)
+        quantize_head(1)
 
-        group_matmuls(3, 0)
-        y_transpose(2, 0, 2, 2)
-        y_transpose(2, 2, 4, 3)
+        group(3, 0)
+        make_addend(3, 2)
         finish(3, 0)
-        y_round(3, 0)
-        y_drain(2, 0, 2, 2)
-        y_drain(2, 2, 4, 3)
-        group_matmuls(3, 1)
-        y_quantize(2, 0, 4)
-        store_words(2 * Q, 3 * Q)
-        store_scales(0, 3 * Q, [nc.sync] * 4)
+        group(3, 1)
+        turn_head(2)
+        make_addend(3, 3)
         finish(3, 1)
-        y_round(3, 1)
-        group_matmuls(3, 2)
+        y_round(3, 0, 1)
+        drain_head(2)
+        group(3, 2)
         finish(3, 2)
         y_round(3, 2)
-        group_matmuls(3, 3)
-        y_transpose(3, 0, 2, 6)
-        y_transpose(3, 2, 3, 7)
-        finish_bf16(3, 3)
-        y_transpose(3, 3, 4, 2)
+        quantize_head(2)
+        store_scales(0, 0, H - 1, [nc.sync] * SCALE_ROWS)
+        group(3, 3)
+
+        pieces = [(0, 2, 6), (2, 3, 7), (3, 4, 2)]
+        y_turn(3, *pieces[0])
+        y_turn(3, *pieces[1])
+        y_round_from_psum(3, 3)
+        y_turn(3, *pieces[2])
         finish(3, 3)
-        y_drain(3, 0, 2, 6)
-        y_drain(3, 2, 3, 7)
-        y_drain(3, 3, 4, 2)
+        for piece in pieces:
+            y_drain(3, *piece)
         y_quantize(3, 0, 2)
         y_quantize(3, 2, 3)
-        store_words(3 * Q, 3 * Q + 3 * P)
+        store_codes(3, 0, 3)
         y_quantize(3, 3, 4)
-        store_words(3 * Q + 3 * P, 4 * Q)
-        store_scales(3 * Q, 4 * Q, [nc.scalar, nc.sync, nc.scalar, nc.sync])
+        store_codes(3, 3, 4)
+        store_scales(1, H - 1, H, [nc.scalar, nc.sync, nc.scalar, nc.sync])

from contextlib import ExitStack

import concourse.mybir as mybir
from concourse.masks import make_identity

Q, H, DH, K, KO = 512, 4, 512, 3584, 512
FLOPS = 2 * Q * (K + KO) * H * DH

F32 = mybir.dt.float32
BF16 = mybir.dt.bfloat16
I32 = mybir.dt.int32
U32 = mybir.dt.uint32
U8 = mybir.dt.uint8
FP8X4 = mybir.dt.float8_e4m3fn_x4
FP4X4 = mybir.dt.float4_e2m1fn_x4
MULT = mybir.AluOpType.mult
ADD = mybir.AluOpType.add

P = 128
TILES = Q // P
K_PASS = 4 * P
MAIN_PASSES = K // K_PASS
PASSES = MAIN_PASSES + 1
PAIRS = PASSES // 2
SCALE_ROWS = 4
FIRST_PASSES = 2
WARM_PASSES = 10

GROUP_BANK = [[0, 1, 2, 3], [4, 5, 6, 7], [2, 3, 6, 7], [0, 1, 4, 5]]
X_BANK = 4
SPARE_BANK = 2


def tile_resampler_query_projection_g5_kernel(
    tc, queries, queries_outlier, wq_words, wq_scales, w_outlier, bias, pos, head_scale, out_0, out_1, out_2
):
    nc = tc.nc
    with ExitStack() as ctx:
        keep = ctx.enter_context(tc.tile_pool(name="keep", bufs=1))
        psum = ctx.enter_context(tc.psum_pool(name="psum", bufs=1))
        ctx.enter_context(tc.manual_schedule())

        def sb(name, shape, dtype):
            return keep.tile(shape, dtype, name=name, align_bytes=64)

        bank = [psum.tile([P, 512], F32, name="bank%d" % i) for i in range(8)]

        ident = sb("ident", [P, P], F32)
        bias_col = sb("bias_col", [P, 16], BF16)
        scale_bf = sb("scale_bf", [P, H], BF16)
        scale = sb("scale", [P, H], F32)
        warm_in = sb("warm_in", [P, 8 * P], BF16)
        warm_codes = sb("warm_codes", [P, 2 * P], U32)
        warm_scales = sb("warm_scales", [P, 2 * P], U8)
        bias_all = sb("bias_all", [P, H, DH], BF16)
        bias_scaled = sb("bias_scaled", [P, H, DH], F32)
        pos_sb = sb("pos_sb", [P, TILES, DH], BF16)
        x_raw = [sb("x_raw%d" % c, [P, 2, 2 * K_PASS], BF16) for c in range(2 * PAIRS)]
        x_halves = [sb("x_halves%d" % i, [P, 4, 2, P], F32) for i in range(2)]
        x_turned = [sb("x_turned%d" % i, [P, 2, 2 * K_PASS], BF16) for i in range(2)]
        x_codes = sb("x_codes", [P, TILES, PASSES * P], U32)
        x_scales = sb("x_scales", [P, TILES, PASSES * P], U8)
        w_codes = [sb("w_codes%d" % h, [P, MAIN_PASSES, 2 * DH], U8) for h in range(H)]
        w_scales_first = sb("w_scales_first", [P, FIRST_PASSES, DH], U8)
        w_scales = [sb("w_scales0", [P, MAIN_PASSES - FIRST_PASSES, DH], U8)]
        w_scales += [sb("w_scales%d" % h, [P, MAIN_PASSES, DH], U8) for h in range(1, H)]
        wo_raw = [sb("wo_raw%d" % h, [P, 4, DH], BF16) for h in range(H)]
        wo_grouped = [sb("wo_grouped%d" % i, [P, DH, 4], BF16) for i in range(2)]
        wo_codes = sb("wo_codes", [P, H, DH], U32)
        wo_scales = sb("wo_scales", [P, H, DH], U8)
        addend = [sb("addend%d" % i, [P, TILES, DH], F32) for i in range(2)]
        y = [sb("y%d" % i, [P, TILES, DH], F32) for i in range(3)]
        y_halves = [sb("y_halves%d" % i, [P, TILES, 2, P, 2], BF16) for i in range(3)]
        y_turned = [sb("y_turned%d" % i, [P, TILES, DH], BF16) for i in range(2)]
        y_codes = sb("y_codes", [P, H * Q], U32)
        y_scales = [sb("y_scales_first", [P, (H - 1) * Q], U8), sb("y_scales_last", [P, Q], U8)]

        x_hbm = queries.rearrange("(a p) k -> p a k", p=P)
        xo_hbm = queries_outlier.rearrange("(a p) k -> p a k", p=P)
        w_codes_hbm = wq_words.bitcast(I32).rearrange("g p c -> p g c")
        w_scales_hbm = wq_scales.bitcast(I32).rearrange("g (q r) c -> r q g c", r=SCALE_ROWS)
        wo_hbm = w_outlier.rearrange("(p t) c -> p t c", t=4)
        y_codes_hbm = out_1[0].rearrange("p m t -> p (m t)").bitcast(I32)
        y_scales_hbm = out_2[0].bitcast(I32).rearrange("(q r) c -> r q c", r=SCALE_ROWS)

        def load_x(pair):
            k0 = 2 * K_PASS * pair
            for half in range(2):
                dst = x_raw[2 * pair + half]
                tiles = slice(2 * half, 2 * half + 2)
                if pair == 0:
                    for a in range(2):
                        nc.sync.dma_start(out=dst[:, a, :], in_=x_hbm[:, 2 * half + a, 0 : 2 * K_PASS])
                elif pair < PAIRS - 1:
                    nc.sync.dma_start(out=dst[:], in_=x_hbm[:, tiles, k0 : k0 + 2 * K_PASS])
                else:
                    nc.sync.dma_start(out=dst[:, :, 0:K_PASS], in_=x_hbm[:, tiles, k0:K])
                    nc.sync.dma_start(out=dst[:, :, K_PASS : 2 * K_PASS], in_=xo_hbm[:, tiles, :])

        def load_w_codes(h, g0, g1):
            cols = slice(DH // 2 * h, DH // 2 * (h + 1))
            nc.sync.dma_start(out=w_codes[h][:].bitcast(I32)[:, g0:g1, :], in_=w_codes_hbm[:, g0:g1, cols])

        def load_w_scales(dst, h, g0, g1):
            cols = slice(DH // 4 * h, DH // 4 * (h + 1))
            for r in range(SCALE_ROWS):
                nc.sync.dma_start(out=dst[:].bitcast(I32)[r:P:32, :, :], in_=w_scales_hbm[r][:, g0:g1, cols])

        def load_wo(h):
            nc.sync.dma_start(out=wo_raw[h][:], in_=wo_hbm[:, :, DH * h : DH * (h + 1)])

        def clear(scale_tile):
            nc.vector.memset(scale_tile[:].bitcast(I32), 0)

        def copy(on_vector, dst, src):
            if on_vector:
                nc.vector.tensor_copy(out=dst, in_=src)
            else:
                nc.scalar.copy(out=dst, in_=src)

        def warm_pass(i):
            nc.tensor.matmul_mx(
                out=bank[SPARE_BANK + i // 2 % 2][:, 2 * P * (i % 2) : 2 * P * (i % 2 + 1)],
                lhsT=warm_codes[:, 0:P].bitcast(FP8X4),
                lhsT_scale=warm_scales[:, 0:P],
                rhs=warm_codes[:].bitcast(FP8X4),
                rhs_scale=warm_scales[:],
                start=True,
                stop=True,
            )

        def spread_bias():
            words = bias_col[:].bitcast(F32)
            dst = bias_all[:].rearrange("p h d -> p (h d)").bitcast(F32).rearrange("p (n j) -> p n j", j=8)
            for b in range(2):
                spare = bank[SPARE_BANK + b]
                for q in range(4):
                    j = 4 * b + q
                    nc.tensor.transpose(
                        spare[:, P * q : P * (q + 1)], words[:, j : j + 1].to_broadcast([P, P]), ident[:]
                    )
                nc.scalar.copy(out=dst[:, :, 4 * b : 4 * b + 4], in_=spare[:].rearrange("p (j n) -> p n j", j=4))

        def x_split(pair, tile, on_vector):
            a = tile % 2
            words = x_raw[2 * pair + tile // 2][:, a : a + 1, :].bitcast(F32)
            src = words.rearrange("p a (g w j) -> p (a g) j w", g=2, j=2)
            copy(on_vector, x_halves[tile // 2][:, 2 * a : 2 * a + 2, :, :], src)

        def x_turn(tile):
            a, dst = tile % 2, bank[X_BANK + tile]
            for g in range(2):
                for j in range(2):
                    q = 2 * g + j
                    nc.tensor.transpose(dst[:, P * q : P * (q + 1)], x_halves[tile // 2][:, 2 * a + g, j, :], ident[:])
            nc.scalar.copy(
                out=x_turned[tile // 2][:, a, :].bitcast(F32).rearrange("p (g u j) -> p g u j", g=2, j=2),
                in_=dst[:].rearrange("p (g j u) -> p g u j", g=2, j=2),
            )

        def x_quantize(pair, tile):
            cols = slice(2 * P * pair, 2 * P * (pair + 1))
            nc.vector.quantize_mx(
                out=x_codes[:, tile, cols].bitcast(FP8X4),
                scales=x_scales[:, tile, cols],
                in_=x_turned[tile // 2][:, tile % 2, :],
            )

        def wo_group(h, c0, c1, on_vector):
            copy(on_vector, wo_grouped[h % 2][:, c0:c1, :], wo_raw[h][:, :, c0:c1].rearrange("p t c -> p c t"))

        def wo_quantize(h):
            nc.vector.quantize_mx(
                out=wo_codes[:, h, :].bitcast(FP8X4),
                scales=wo_scales[:, h, :],
                in_=wo_grouped[h % 2][:].rearrange("p c t -> p (c t)"),
            )

        def mx_pass(h, tile, g):
            if g == MAIN_PASSES:
                rhs, rhs_scale = wo_codes[:, h, :].bitcast(FP8X4), wo_scales[:, h, :]
            else:
                rhs = w_codes[h][:, g, :].bitcast(FP4X4)
                if h > 0:
                    rhs_scale = w_scales[h][:, g, :]
                elif g < FIRST_PASSES:
                    rhs_scale = w_scales_first[:, g, :]
                else:
                    rhs_scale = w_scales[0][:, g - FIRST_PASSES, :]
            nc.tensor.matmul_mx(
                out=bank[GROUP_BANK[h][tile]][:],
                lhsT=x_codes[:, tile, P * g : P * (g + 1)].bitcast(FP8X4),
                lhsT_scale=x_scales[:, tile, P * g : P * (g + 1)],
                rhs=rhs,
                rhs_scale=rhs_scale,
                start=(g == 0),
                stop=(g == PASSES - 1),
            )

        def head0_pair(pair, tile):
            for g in range(2 * pair, min(2 * pair + 2, MAIN_PASSES)):
                mx_pass(0, tile, g)

        def sweep(h, g0, g1):
            for g in range(g0, g1):
                for tile in range(TILES):
                    mx_pass(h, tile, g)

        def group(h, tile):
            for g in range(PASSES):
                mx_pass(h, tile, g)

        def scale_bias(h):
            nc.vector.tensor_scalar(
                out=bias_scaled[:, h, :], in0=bias_all[:, h, :], scalar1=scale[:, h : h + 1], scalar2=None, op0=MULT
            )

        def multiply_add(h, dst, in0, in1):
            nc.vector.scalar_tensor_tensor(out=dst, in0=in0, scalar=scale[:, h : h + 1], in1=in1, op0=MULT, op1=ADD)

        def make_addend(h, *tiles):
            for tile in tiles:
                multiply_add(h, addend[h % 2][:, tile, :], pos_sb[:, tile, :], bias_scaled[:, h, :])

        def finish(h, *tiles):
            for tile in tiles:
                dst = y[h % 3][:, tile, :]
                multiply_add(h, dst, bank[GROUP_BANK[h][tile]][:], addend[h % 2][:, tile, :])
                nc.sync.dma_start(out=out_0[h, P * tile : P * (tile + 1), :], in_=dst)

        def by_halves(ap):
            return ap.rearrange("p (w j e) -> p j w e", j=2, e=2)

        def y_round(h, *tiles):
            for tile in tiles:
                nc.scalar.copy(out=y_halves[h % 3][:, tile, :, :, :], in_=by_halves(y[h % 3][:, tile, :]))

        def y_round_from_psum(h, tile):
            sums, add = by_halves(bank[GROUP_BANK[h][tile]][:]), by_halves(addend[h % 2][:, tile, :])
            for j in range(2):
                multiply_add(h, y_halves[h % 3][:, tile, j, :, :], sums[:, j, :, :], add[:, j, :, :])

        def y_turn(h, t0, t1, b):
            for tile in range(t0, t1):
                for j in range(2):
                    q = 2 * (tile - t0) + j
                    words = y_halves[h % 3][:, tile, j, :, :].rearrange("p w e -> p (w e)").bitcast(F32)
                    nc.tensor.transpose(bank[b][:, P * q : P * (q + 1)], words, ident[:])

        def y_drain(h, t0, t1, b):
            nc.scalar.copy(
                out=y_turned[h % 2][:, t0:t1, :].bitcast(F32).rearrange("p a (u j) -> p a u j", j=2),
                in_=bank[b][:, 0 : 2 * P * (t1 - t0)].rearrange("p (a j u) -> p a u j", a=t1 - t0, j=2),
            )

        def y_quantize(h, t0, t1):
            last = h // (H - 1)
            c0, c1, base = Q * h + P * t0, Q * h + P * t1, (H - 1) * Q * last
            nc.vector.quantize_mx(
                out=y_codes[:, c0:c1].bitcast(FP8X4),
                scales=y_scales[last][:, c0 - base : c1 - base],
                in_=y_turned[h % 2][:, t0:t1, :].rearrange("p a c -> p (a c)"),
            )

        def store_codes(h, t0, t1):
            cols = slice(Q * h + P * t0, Q * h + P * t1)
            nc.sync.dma_start(out=y_codes_hbm[:, cols], in_=y_codes[:, cols].bitcast(I32))

        def store_scales(last, h0, h1, queues):
            cols = slice(Q // 4 * h0, Q // 4 * h1)
            for r in range(SCALE_ROWS):
                queues[r].dma_start(out=y_scales_hbm[r][:, cols], in_=y_scales[last][:].bitcast(I32)[r:P:32, :])

        def head_banks(h):
            return [(0, 2, [0, 4, 2][h]), (2, 4, [1, 5, 3][h])]

        def turn_head(h):
            for t0, t1, b in head_banks(h):
                y_turn(h, t0, t1, b)

        def drain_head(h):
            for t0, t1, b in head_banks(h):
                y_drain(h, t0, t1, b)

        def quantize_head(h):
            y_quantize(h, 0, TILES)
            store_codes(h, 0, TILES)

        make_identity(nc, ident[:])
        nc.gpsimd.dma_start(out=bias_col[:], in_=bias.rearrange("(p j) -> p j", p=P))
        nc.vector.memset(warm_in[:].bitcast(I32), 0)
        clear(w_scales_first)
        nc.vector.quantize_mx(out=warm_codes[:].bitcast(FP8X4), scales=warm_scales[:], in_=warm_in[:])
        clear(w_scales[0])
        clear(w_scales[1])

        load_x(0)
        load_w_scales(w_scales_first, 0, 0, FIRST_PASSES)
        load_w_codes(0, 0, 2)
        load_x(1)
        load_w_scales(w_scales[0], 0, FIRST_PASSES, MAIN_PASSES)
        load_w_codes(0, 2, 4)
        load_x(2)
        load_w_codes(0, 4, MAIN_PASSES)
        load_x(3)
        load_w_scales(w_scales[1], 1, 0, MAIN_PASSES)
        load_w_codes(1, 0, 3)
        nc.sync.dma_start(out=scale_bf[:], in_=head_scale.partition_broadcast(P))
        load_wo(0)
        nc.sync.dma_start(out=pos_sb[:], in_=pos.rearrange("(a p) d -> p a d", p=P))
        load_w_codes(1, 3, MAIN_PASSES)
        load_wo(1)

        for i in range(WARM_PASSES):
            warm_pass(i)

        for tile in range(TILES):
            x_split(0, tile, True)
        for pair in range(PAIRS):
            first, last = pair == 0, pair == PAIRS - 1
            for tile in range(TILES):
                x_turn(tile)
                if first and tile < 2:
                    warm_pass(tile)
            if first:
                spread_bias()
            else:
                head0_pair(pair - 1, 2)
                head0_pair(pair - 1, 3)
            for tile in range(2):
                x_quantize(pair, tile)
                head0_pair(pair, tile)
                if last:
                    mx_pass(1, tile, 0)
            if not last:
                for tile in range(3):
                    x_split(pair + 1, tile, True)
            x_quantize(pair, 2)
            if not last:
                x_split(pair + 1, 3, False)
            x_quantize(pair, 3)
            if pair < 2:
                clear(w_scales[2 + pair])
        for tile in range(2, TILES):
            head0_pair(PAIRS - 1, tile)
            mx_pass(1, tile, 0)

        load_w_scales(w_scales[2], 2, 0, MAIN_PASSES)
        load_wo(2)
        load_w_codes(2, 0, 3)
        load_w_codes(2, 3, MAIN_PASSES)
        load_w_scales(w_scales[3], 3, 0, MAIN_PASSES)
        load_wo(3)
        load_w_codes(3, 0, MAIN_PASSES)


        nc.vector.tensor_copy(out=scale[:], in_=scale_bf[:])
        for h in range(H - 1):
            scale_bias(h)
        wo_group(0, 0, DH // 2, False)
        wo_group(0, DH // 2, DH, True)
        make_addend(0, 2)
        wo_quantize(0)
        make_addend(0, 3, 0, 1)
        sweep(1, 1, 4)
        sweep(0, MAIN_PASSES, PASSES)
        sweep(1, 4, MAIN_PASSES)
        wo_group(1, 0, DH, False)
        finish(0, 2, 3)
        make_addend(1, 0)
        wo_quantize(1)
        finish(0, 0, 1)
        sweep(1, MAIN_PASSES, PASSES)
        wo_group(2, 0, DH, False)
        y_round(0, 0, 1)
        make_addend(1, 1, 2)
        wo_quantize(2)
        y_round(0, 2, 3)
        make_addend(1, 3)

        finish(1, 2, 3, 0, 1)
        y_round(1, 0, 1, 2, 3)
        for tile in range(3):
            group(2, tile)
        turn_head(0)
        turn_head(1)
        make_addend(2, 0, 1)
        finish(2, 0, 1)
        make_addend(2, 2)
        scale_bias(3)
        wo_group(3, 0, DH, False)
        make_addend(2, 3)
        finish(2, 2)
        drain_head(0)
        drain_head(1)
        make_addend(3, 0)
        wo_quantize(3)
        group(2, 3)
        make_addend(3, 1)
        quantize_head(0)
        finish(2, 3)
        y_round(2, 0, 1, 2, 3)
        quantize_head(1)

        group(3, 0)
        make_addend(3, 2)
        finish(3, 0)
        group(3, 1)
        turn_head(2)
        make_addend(3, 3)
        finish(3, 1)
        y_round(3, 0, 1)
        drain_head(2)
        group(3, 2)
        finish(3, 2)
        y_round(3, 2)
        quantize_head(2)
        store_scales(0, 0, H - 1, [nc.sync] * SCALE_ROWS)
        group(3, 3)

        pieces = [(0, 2, 6), (2, 3, 7), (3, 4, 2)]
        y_turn(3, *pieces[0])
        y_turn(3, *pieces[1])
        y_round_from_psum(3, 3)
        y_turn(3, *pieces[2])
        finish(3, 3)
        for piece in pieces:
            y_drain(3, *piece)
        y_quantize(3, 0, 2)
        y_quantize(3, 2, 3)
        store_codes(3, 0, 3)
        y_quantize(3, 3, 4)
        store_codes(3, 3, 4)
        store_scales(1, H - 1, H, [nc.scalar, nc.sync, nc.scalar, nc.sync])
